import numpy as np, ml_dtypes
CORES = [24,25,26,27,28,29,30,31]
N = 8
BF = ml_dtypes.bfloat16
def gentries(a):
    return np.ascontiguousarray(a.reshape(8, 16, -1).transpose(0, 2, 1)).reshape(8, -1)
def gtable(e):
    e = np.asarray(e); return np.ascontiguousarray(e.reshape(8, -1, 16).transpose(0, 2, 1)).reshape(128, -1).astype(np.int32)
V, S, L, DS = 2048, 256, 8, (1, 6, 4)
W = N * V
def mix(rng, a):
    return np.take_along_axis(a, np.argsort(rng.random(a.shape), axis=-1), -1)
def some(rng, pool, shape, n):
    q = len(pool) // n
    return pool[np.arange(n) * q + rng.integers(0, q, shape + (n,))]
def parts(rng):
    x = (256 * np.sqrt(rng.random((N, 8, 1, V))) * rng.random((N, 8, 16, V))).astype(np.int64)
    sl = np.empty((N, 8, S, L), np.int64)
    for g in range(8):
        p = rng.permutation(W); a = p[:3 * L][np.argsort(rng.random((N, S, 3 * L)), axis=-1)[..., :L]]
        sl[:, g] = np.where(np.arange(L) < rng.integers(0, L + 1, (N, S, 1)), a, some(rng, p[3 * L:], (N, S), L))
    return x, mix(rng, sl), rng.integers(0, S * L, (N, 8, V))
def pack(x, sl, pr):
    return {"x": np.ascontiguousarray(x.reshape(N, 128, V)).astype(np.float32).astype(BF), "sl": np.stack([gtable(a.reshape(8, -1)) for a in sl]), "prey": np.stack([gtable(a) for a in pr])}
def setup_inputs(rng):
    return pack(*parts(rng))
def setup_inputs_pools(rng):
    x, sl, pr = parts(rng)
    for g in range(8):
        x[:, g] = rng.integers(0, 256, 16)[np.argsort(rng.random((N, 16, V)), axis=1)]
    ms = np.array([0, 1, 2, L // 2, L - 1, L])
    for a in range(N):
        b = a ^ DS[0]
        if a < b:
            for g in range(8):
                e = some(rng, rng.permutation(W), (S,), 2 * L); m = rng.choice(ms, (S, 1)); m[:6, 0] = ms
                if g == 2: m[:] = 0
                if g == 5: m[:] = L
                sl[a, g] = mix(rng, e[:, :L]); sl[b, g] = mix(rng, np.where(np.arange(L) < m, e[:, L:], e[:, :L]))
    return pack(x, sl, pr)
def setup_inputs_ties(rng):
    x, sl, pr = parts(rng)
    kind = rng.integers(0, 4, (N, 8, V)); proto = rng.integers(0, 256, (8, 16, 4))
    proto[1, :, 1] = proto[1, ::-1, 0]; proto[1, :, 3] = proto[1, ::-1, 2]; proto[0] = rng.integers(0, 256, (1, 1))
    for q in range(N):
        for g in range(8): x[q, g] = proto[g][:, kind[q, g]]
    return pack(x, sl, pr)
def setup_inputs_few(rng):
    x, sl, pr = parts(rng); o = rng.permutation(N)
    for g in (0, 4):
        c = np.concatenate([np.array([0, W - 1]), 1 + rng.permutation(W - 2)[:L]])
        sl[:, g] = c[np.argsort(rng.random((N, S, L + 2)), axis=-1)[..., :L]]
    pr[:, 1] = rng.choice(np.array([0, L - 1, L, S * L - 1]), (N, V)); pr[:, 5] = S * L - 1
    sl[1:, 5] = sl[0, 5]
    sl[:, 2] = mix(rng, some(rng, o[0] * V + rng.permutation(V), (N, S), L))
    sl[:, 6] = mix(rng, some(rng, o[1] * V + 1024 * rng.integers(0, V // 1024) + rng.permutation(1024), (N, S), L))
    for g in (3, 7): sl[:, g] = mix(rng, np.zeros((N, S, 1), np.int64) + rng.permutation(W)[:L])
    return pack(x, sl, pr)
def setup_inputs_ends(rng):
    x, sl, pr = parts(rng); x = 255 * rng.integers(0, 2, x.shape)
    for g in (0, 3, 6): x[:, g, :, 0::2] = 0; x[:, g, :, 1::2] = 255
    x[:, 1, :, 0::2] = rng.integers(0, 32, (N, 16, V // 2)); x[:, 1, :, 1::2] = rng.integers(224, 256, (N, 16, V // 2))
    c = np.arange(V); low = 255 * (L - 1) // (2 * L - 1); e = rng.integers(0, 4, (N, 16, V))
    x[:, 2] = np.where(np.arange(16)[:, None] % L == (c // 2) % L, 255 * (1 - c % 2), np.where(c % 2 == 1, 255 - low + e, low - e))
    for a in range(N):
        odd = int(a > (a ^ DS[0]))
        sl[a, 0] = some(rng, 2 * rng.permutation(W // 2) + odd, (S,), L); sl[a, 3] = some(rng, 2 * rng.permutation(W // 2) + 1 - odd, (S,), L)
        sl[a, 1] = some(rng, 2 * rng.permutation(W // 2) + odd, (S,), L)
        sl[a, 2] = mix(rng, 2 * (L * rng.integers(0, W // (2 * L), (S, L)) + np.arange(L)) + odd)
    t = np.arange(S)
    for a in range(N):
        b = a ^ DS[0]
        if a < b: sl[b, 0, t, rng.integers(0, L, S)] = sl[a, 0, t, rng.integers(0, L, S)]
    sl[:, 4] = np.concatenate([rng.permutation(W) for i in range((N * S * L + W - 1) // W)])[:N * S * L].reshape(N, S, L)
    one = rng.integers(0, N) * V + np.concatenate([rng.permutation(V) for i in range((S * L + V - 1) // V)])[:S * L].reshape(S, L)
    sl[:, 5] = mix(rng, np.zeros((N, 1, 1), np.int64) + one)
    sl[:, 7] = mix(rng, some(rng, 16 * rng.permutation(W // 16) + rng.integers(0, 16), (N, S), L))
    for g in (4, 5): pr[:, g] = mix(rng, np.zeros((N, 1), np.int64) + np.arange(max(V, S * L)) % (S * L))[:, :V]
    return pack(x, sl, pr)
def setup_inputs_spread(rng):
    x, sl, pr = parts(rng)
    x = (np.exp2(8 * rng.random((N, 8, 1, V))) * rng.random((N, 8, 16, V)) * (rng.random((N, 8, 1, V)) > 0.0625)).astype(np.int64)
    pr = np.minimum((S * L * rng.random((N, 8, V)) ** 3).astype(np.int64), S * L - 1)
    return pack(x, sl, pr)
def check_inputs(d):
    bad = []
    v = np.asarray(d["x"]).astype(np.float32)
    if not np.all((v >= 0) & (v <= 255) & (v == np.floor(v))): bad.append("range of x")
    for k, hi in (("sl", W - 1), ("prey", S * L - 1)):
        if np.min(d[k]) < 0 or np.max(d[k]) > hi: bad.append("range of " + k)
    e = np.sort(np.stack([gentries(a) for a in d["sl"]]).reshape(N, 8, S, L), axis=-1)
    if np.any(e[..., 1:] == e[..., :-1]): bad.append("different species in a site of sl")
    return bad
def reference(x, sl, prey):
    v = x.astype(np.float32).astype(np.int64).reshape(N, 8, 16, V)
    ls = np.stack([gentries(a) for a in sl]).astype(np.int64).reshape(N, 8, S, L); pl = np.stack([gentries(a) for a in prey]).astype(np.int64)
    j = np.arange(L)
    for d in DS:
        w = np.concatenate([v[a] for a in range(N)], axis=2)
        cs, od = [], []
        for a in range(N):
            c = np.add.reduce(np.take_along_axis(w, ls[a].reshape(8, 1, S * L), 2).reshape(8, 16, S, L), axis=3)
            cs.append(c); od.append(np.argsort(np.arange(S) - S * np.add.reduce(c, axis=1), axis=1))
        new = np.array(ls)
        for a in range(N):
            b = a ^ d
            if a < b:
                la = np.take_along_axis(ls[a], od[a][:, :, None], 1); lb = np.take_along_axis(ls[b], od[b][:, :, None], 1)
                ca = np.take_along_axis(cs[a], od[a][:, None, :], 2)[..., None]; cb = np.take_along_axis(cs[b], od[b][:, None, :], 2)[..., None]
                pool = np.concatenate([la, lb], axis=2)
                px = L * np.take_along_axis(w, pool.reshape(8, 1, -1), 2).reshape(8, 16, S, 2 * L)
                key = 2 * L * np.add.reduce(np.abs(px - ca) - np.abs(px - cb), axis=1) + np.arange(2 * L)
                eq = la[:, :, :, None] == lb[:, :, None, :]
                com = np.concatenate([np.any(eq, axis=3), np.any(eq, axis=2)], axis=2)
                m = np.add.reduce((~com[:, :, :L]).astype(np.int64), axis=2)[:, :, None]
                sp = np.take_along_axis(pool, np.argsort(np.where(com, 2 ** 40 + np.arange(2 * L), key), axis=2), 2)
                np.put_along_axis(new[a], od[a][:, :, None], np.take_along_axis(sp, np.where(j < m, j, m + j), 2), 1)
                np.put_along_axis(new[b], od[b][:, :, None], np.take_along_axis(sp, np.where(j < m, m + j, L + j), 2), 1)
        ls = new
        hx = [np.take_along_axis(w, np.take_along_axis(ls[a].reshape(8, S * L), pl[a], 1)[:, None, :], 2) for a in range(N)]
        v = (v + np.stack(hx) + 1) >> 1
    return {"yl": np.stack([gtable(a.reshape(8, -1)) for a in ls]).astype(np.float32), "yx": v.reshape(N, 128, V).astype(np.float32)}

@@ -1,0 +1,547 @@
+from concourse.bass import DstId, RemoteDMATransfer
+from concourse.mybir import AluOpType as A, ActivationFunctionType as F
+
+DS = (1, 6, 4)
+OUTW = (1024, 512, 512)
+DMA0 = (5, 6, 7)
+DMAB = {1: (0, (5, 6, 7)), 2: (2, (5, 6, 7))}
+NV = (8, 8, 8)
+MAGIC = 12582912.0
+f32, bf, f16, i32, u16 = "float32", "bfloat16", "float16", "int32", "uint16"
+
+SCRATCH = {
+    "stx": ("dram", [8, 128, 256], bf), "ldx": ("dram", [8, 128, 256], bf),
+    "sts": ("dram", [8, 128, 16], i32), "lds": ("dram", [8, 128, 16], i32),
+    "stp": ("dram", [8, 128, 16], i32), "ldp": ("dram", [8, 128, 16], i32),
+    "stl": ("dram", [8, 128, 16], f32), "ldl": ("dram", [8, 128, 16], f32),
+    "Mall": ("sbuf", [128, 32, 8, 16], bf),
+}
+for _k, _w in enumerate(OUTW):
+    SCRATCH["sto%d" % _k] = ("dram", [8, 128, _w // 8], bf)
+    SCRATCH["ldo%d" % _k] = ("dram", [8, 128, _w // 8], bf)
+for _k in range(8):
+    SCRATCH["B%d" % _k] = ("psum", [128, 512], f32)
+for _n, _w, _d in (
+    ("TT", 16384, bf), ("X", 2048, bf), ("Xn", 2048, f32), ("N16", 2048, f16), ("M1", 2048, f16), ("M2", 2048, f16),
+    ("FF", 4096, f16), ("SL", 128, i32), ("PR", 128, i32), ("prU", 128, u16), ("offU", 128, u16),
+    ("t1", 128, i32), ("t2", 128, i32), ("t3", 128, i32), ("t4", 128, i32), ("dh", 128, bf), ("dl", 128, bf),
+    ("IDd", 256, bf), ("IDs", 256, bf), ("Z", 256, f32), ("C16", 256, f16), ("Zs", 256, f32), ("od", 256, bf),
+    ("Cps", 256, f32), ("Cp", 256, f32), ("neg", 16, f32), ("posU", 16, u16), ("ordU", 16, u16),
+    ("Kf", 256, f32), ("Ks", 256, f32), ("AB", 512, f32), ("Eq", 512, bf), ("com", 256, bf),
+    ("sg", 1024, bf), ("Tq", 256, f32), ("Rq", 256, f32), ("vv", 512, f16), ("Ns", 256, bf), ("YL", 128, f32),
+    ("i256", 256, f32), ("i144", 144, f32), ("cgrp", 128, f32), ("prow", 256, f32), ("trow", 256, f32), ("prow16", 512, f16),
+    ("qrow", 512, f16), ("zrow", 16, f16), ("XH", 1024, bf), ("Ih", 128, bf),
+    ("pi", 8, i32), ("pj", 8, i32), ("cols", 64, f32),
+    ("IW", 256, bf), ("I8", 128, bf), ("BWp", 144, f16), ("BWn", 144, f16), ("BWb", 144, bf), ("blk", 128, bf), ("KR", 1024, f16),
+    ("G8", 8, f32), ("G8h", 8, f16), ("on16", 128, f16), ("onb", 8, bf), ("z32", 256, f32), ("zb", 256, bf),
+    ("SM", 768, bf), ("WW", 768, bf), ("Perm", 408, f32), ("D2", 768, bf), ("KD", 1536, f32),
+    ("DGp", 1152, bf), ("KDb", 512, bf), ("KC", 1536, bf), ("RM", 1536, bf), ("CM", 768, bf),
+):
+    SCRATCH[_n] = ("sbuf", [128, _w], _d)
+
+SEMAPHORES = ["cV", "cS", "cP", "cG", "sent", "ax", "al", "ayl", "dx", "dxo", "ds", "dso", "dp", "dpo", "dt0", "dsl", "dpr",
+              "dT0", "dT1", "dT2", "dl", "dlo", "dyl"] + ["%s%d" % (a, k) for a in ("ao", "do", "doo", "dy") for k in range(len(OUTW))]
+
+
+def V(name, c0=0, c1=None, st=1, p0=0, p1=128):
+    return ("c", name, p0, p1, c0, SCRATCH[name][1][1] if c1 is None else c1, st)
+
+
+def M(b0, b1, r0, r1):
+    return ("m", "Mall", r0, r1, b0, b1, 1)
+
+
+def D(name, s0=0, s1=8):
+    return ("d", name, s0, s1, 0, 1, 1)
+
+
+def E(name, p0=0, p1=128, c0=None, c1=None):
+    return ("e", name, p0, p1, c0, c1, 1)
+
+
+def I(win, off):
+    return ("i", win, off)
+
+
+def regions(a):
+    if a[0] == "i":
+        return [a[1], a[2]]
+    return [] if a[0] == "e" else [a]
+
+
+def meet(a, b):
+    return a[1] == b[1] and a[2] < b[3] and b[2] < a[3] and a[4] < b[5] and b[4] < a[5]
+
+
+def rank_program(g, core, T, topo):
+    me = T.rank_of(core)
+    if me is None:
+        return
+    ops = []
+
+    def ap(a):
+        if not isinstance(a, tuple):
+            return a
+        if a[0] == "i":
+            return ap(a[1]).indirect(ap(a[2]))
+        t = T[a[1]]
+        if a[0] == "c":
+            return t[a[2]:a[3], a[4]:a[5]] if a[6] == 1 else t[a[2]:a[3], a[4]:a[5]:a[6]]
+        if a[0] == "m":
+            return t[:, a[4]] if a[5] == a[4] + 1 else t[:, a[4]:a[5], a[2], :]
+        if a[0] == "d":
+            return t[a[2]] if a[3] == a[2] + 1 else t[a[2]:a[3]]
+        return t[a[2]:a[3], :] if a[4] is None else t[a[2]:a[3], a[4]:a[5]]
+
+    def rec(q, fn, out, ins, sem=None, inc=0):
+        wr, rd = [], []
+        if out[0] == "i":
+            wr.append(out[1]); rd.append(out[2])
+        else:
+            wr += regions(out)
+        for a in ins:
+            if isinstance(a, tuple):
+                rd += regions(a)
+        ops.append({"q": q, "fn": fn, "wr": wr, "rd": rd, "sem": sem, "inc": inc})
+
+    def mm(out, l, r, start=True, stop=True):
+        rec("P", lambda: g.tensor.matmul(ap(out), ap(l), ap(r), start, stop), out, [l, r])
+
+    def mms(out, pairs, start=True, stop=True):
+        for k, (l, r) in enumerate(pairs):
+            mm(out, l, r, start and k == 0, stop and k == len(pairs) - 1)
+
+    def cp(out, a):
+        rec("V", lambda: g.vector.tensor_copy(ap(out), ap(a)), out, [a])
+
+    def tt(out, a, b, op):
+        rec("V", lambda: g.vector.tensor_tensor(ap(out), ap(a), ap(b), op), out, [a, b])
+
+    def ts(out, a, s1, op0, s2=None, op1=None):
+        if op1 is None:
+            rec("V", lambda: g.vector.tensor_scalar(ap(out), ap(a), ap(s1), None, op0), out, [a, s1])
+        else:
+            rec("V", lambda: g.vector.tensor_scalar(ap(out), ap(a), ap(s1), ap(s2), op0, op1), out, [a, s1, s2])
+
+    def ms(out, v):
+        rec("V", lambda: g.vector.memset(ap(out), v), out, [])
+
+    def act(out, a, fn=F.Identity, bias=0.0, scale=1.0):
+        rec("S", lambda: g.scalar.activation(ap(out), ap(a), fn, bias=ap(bias), scale=ap(scale)), out, [a, bias, scale])
+
+    def iota(out, pat, base=0, cm=0, flt=True):
+        if flt:
+            rec("G", lambda: g.iota(ap(out), pat, base, cm, allow_small_or_imprecise_dtypes=True), out, [])
+        else:
+            rec("G", lambda: g.iota(ap(out), pat, base, cm), out, [])
+
+    def mark(out, a, pat, base, fill):
+        rec("G", lambda: g.affine_select(ap(out), ap(a), pat, A.not_equal, float(fill), base, 1), out, [a])
+
+    def dma(q, out, a, sem):
+        eng = {"Y": g.sync, "S": g.scalar, "G": g}[q]
+        rec(q, lambda: eng.dma_start(ap(out), ap(a)), out, [a], sem, 16)
+
+    far = [r for r in range(8) if r != me and topo.die(T.cores[r]) != topo.die(core)]
+    near = [r for r in range(8) if r != me and topo.die(T.cores[r]) == topo.die(core)]
+    peers = []
+    while far or near:
+        peers += far[:1] + near[:1]
+        far, near = far[1:], near[1:]
+
+    def send(pairs, sem):
+        trs = []
+        for n, (st, ld) in enumerate(pairs):
+            for k, r in enumerate(peers):
+                en = topo.engines(core, T.cores[r])
+                h = len(en) // 2
+                m = (1 << en[k]) | (1 << en[k + h]) if len(pairs) == 1 else 1 << en[k + n * h]
+                rid, pid = topo.addr(T.cores[r])[:2]
+                trs.append((rid, pid, m, st, r, ld))
+        fn = lambda: g.remote_dma_fused([RemoteDMATransfer(dst_ids=[DstId(rid=a, pnc=b)], dma_engine_mask=m, remote_sem=T.sem[sem],
+                                                           src=T[st][r], dst=T[ld][me]) for a, b, m, st, r, ld in trs],
+                                        local_sem=T.sem["sent"])
+        ops.append({"q": "G", "fn": fn, "wr": [], "rd": [D(st, r, r + 1) for st, ld in pairs for r in peers], "sem": "sent", "inc": 14, "remote": 1})
+        ops.append({"q": "R", "fn": None, "wr": [D(ld, r, r + 1) for st, ld in pairs for r in peers], "rd": [], "sem": sem, "inc": 14})
+
+    B = lambda k, c0=0, c1=512, st=1: V("B%d" % k, c0, c1, st)
+    cnames = {}
+
+    def col(n):
+        if n not in cnames:
+            cnames[n] = len(cnames)
+        return V("cols", cnames[n], cnames[n] + 1)
+
+    r0, r1 = 16 * me, 16 * me + 16
+    dma("Y", D("stx"), E("x"), "dx")
+    dma("S", D("sts"), E("sl"), "ds")
+    dma("G", D("stp"), E("prey"), "dp")
+    dma("Y", D("ldx", me, me + 1), E("x", r0, r1), "dxo")
+    dma("S", D("lds", me, me + 1), E("sl", r0, r1), "dso")
+    dma("S", D("ldp", me, me + 1), E("prey", r0, r1), "dpo")
+    iota(V("pi", 0, 1), [[0, 1]], 0, 1, False)
+    iota(V("i256"), [[0, 2], [1, 128]])
+    iota(V("i144"), [[1, 144]])
+    iota(V("cgrp"), [[1, 8], [0, 16]])
+    send([("sts", "lds"), ("stp", "ldp")], "al")
+    send([("stx", "ldx")], "ax")
+    iota(V("prow"), [[1, 256]])
+    dma("Y", V("SL"), D("lds"), "dsl")
+    dma("Y", V("PR"), D("ldp"), "dpr")
+    dma("Y", V("TT", 0, 2048), D("ldx"), "dt0")
+    for b in DMA0:
+        dma("Y", V("TT", 2048 * b, 2048 * b + 2048, p1=128 - 16 * b), D("ldx", b, 8), "dT0")
+        dma("Y", V("TT", 2048 * b, 2048 * b + 2048, p0=128 - 16 * b), D("ldx", 0, b), "dT0")
+
+    ms(V("z32"), 0.0); ms(V("zb"), 0.0); ms(V("on16"), 1.0); ms(V("onb"), 1.0)
+    for n in range(3):
+        ms(V("Perm", 136 * n, 136 * n + 8), 0.0)
+    ms(V("qrow", p1=1), 0.25); ms(V("zrow", p1=1), 0.0); ms(V("Zs"), 0.0)
+    pi = V("pi", 0, 1)
+    pj = lambda k: V("pj", k, k + 1)
+    ts(pj(0), pi, 4, A.arith_shift_right)
+    ts(pj(1), pi, 7, A.bitwise_and)
+    ts(pj(2), pi, 15, A.bitwise_and)
+    ts(pj(3), pi, 4, A.arith_shift_right, 1, A.bitwise_and)
+    ts(pj(4), pi, 6, A.arith_shift_right)
+    ts(pj(5), pi, 31, A.bitwise_and)
+    for n in ("grp", "j", "i", "sd0", "sd1", "p31"):
+        col(n)
+    cp(V("cols", 0, 6), V("pj", 0, 6))
+    cp(col("p"), pi)
+    ts(V("IW"), V("i256"), col("p"), A.is_equal)
+    ts(col("mlo"), col("i"), 8.0, A.is_lt)
+    ts(col("mhi"), col("i"), 8.0, A.is_ge)
+    ts(col("m8"), col("i"), 8.0, A.is_equal)
+    ts(col("mlo128"), col("i"), 8.0, A.is_lt, 128.0, A.mult)
+    ts(col("rot"), col("grp"), -2048.0, A.mult, 16384.0, A.add)
+    ts(col("g15"), col("grp"), 16.0, A.mult, 15.0, A.add)
+    ts(col("psc"), col("grp"), 2.5, A.is_lt, 0.5, A.mult)
+    ts(col("pbi"), col("grp"), 2.5, A.is_gt, 127.5, A.mult)
+    ts(col("w4"), col("p31"), 24.0, A.is_ge, col("sd1"), A.mult)
+    ts(V("G8"), V("i144", 0, 8), col("grp"), A.is_equal, -2048.0, A.mult)
+    ts(V("blk"), V("cgrp"), col("grp"), A.is_equal)
+    ts(col("psc"), col("psc"), 0.5, A.add)
+    ts(col("w4"), col("w4"), -32.0, A.mult, 64.0, A.add)
+    ts(V("BWp"), V("i144"), col("g15"), A.is_equal)
+    ts(V("BWb"), V("i144"), col("g15"), A.is_equal)
+    ts(V("BWn"), V("i144"), col("g15"), A.is_equal, -1.0, A.mult)
+    cp(V("G8h"), V("G8"))
+    for r in range(8):
+        ts(V("KR", 128 * r, 128 * r + 128), V("on16"), V("G8", r, r + 1), A.mult)
+    I0, Iup, Idn = V("IW", 0, 128), V("IW", 8, 136), V("IW", 120, 248)
+    SM = lambda k: V("SM", 128 * k, 128 * k + 128)
+    OH, OL, S1, L1, H0, H1 = [SM(k) for k in range(6)]
+    act(V("I8"), I0, scale=0.125)
+    act(V("Ih"), I0, scale=0.5)
+    for o, a, c in ((OH, I0, "mlo"), (OL, Iup, "mhi"), (S1, Idn, "mlo"), (L1, I0, "mhi"), (H0, I0, "mlo128"), (H1, Idn, "mlo128")):
+        act(o, a, scale=col(c))
+    for y in "01":
+        sd = col("sd" + y)
+        ts(col("sig" + y), sd, -256.0, A.mult, 128.0, A.add)
+        ts(col("q" + y), sd, 8.0, A.mult, col("j"), A.add)
+        ts(col("be" + y), sd, 9.0, A.mult, col("j"), A.add)
+        ts(col("cA" + y), sd, -1024.0, A.mult, 1024.0, A.add)
+        ts(col("nb" + y), col("j"), -1920.0, A.mult, -1920.0, A.add)
+        ts(col("q" + y), col("q" + y), col("mlo"), A.mult)
+        ts(col("be" + y), col("be" + y), -8.0, A.add, col("mlo128"), A.mult)
+        ts(col("s1" + y), col("cA" + y), col("mlo"), A.mult)
+        ts(col("s3" + y), col("cA" + y), -64.0, A.add, col("m8"), A.mult)
+        ts(col("de" + y), col("sig" + y), col("mlo"), A.mult, 1.0 / 16384, A.mult)
+        ts(col("nb" + y), sd, 1024.0, A.mult, col("nb" + y), A.add)
+        ts(col("be" + y), col("be" + y), 8192.0, A.mult)
+        ts(col("s2" + y), col("s1" + y), -0.125, A.mult, col("s3" + y), A.add)
+    WW = lambda y, k: V("WW", 384 * int(y) + 128 * k, 384 * int(y) + 128 * k + 128)
+    for y in "01":
+        act(WW(y, 0), I0, scale=col("s1" + y))
+        act(WW(y, 1), V("blk"), scale=col("s2" + y))
+        act(WW(y, 2), I0, scale=col("de" + y))
+    cp(V("prow16", 0, 256, p1=1), V("prow", p1=1))
+    cp(V("prow16", 256, 512, p1=1), V("prow", p1=1))
+    ts(V("trow"), V("prow"), 256.0, A.mult, -127.875, A.add)
+
+    def maps(n):
+        d = DS[n]
+        ra = [r for r in range(8) if r < r ^ d]
+        rb = [r ^ d for r in ra]
+        pat, base = [[-1, 16]], 0
+        for k in range(3):
+            if d >> k & 1:
+                pat.insert(0, [16 << k, 2]); base -= 16 << k
+            elif pat[0][0] < 0 and -pat[0][0] * pat[0][1] == 16 << k:
+                pat[0] = [pat[0][0], pat[0][1] * 2]
+            else:
+                pat.insert(0, [-(16 << k), 2])
+        mark(V("Perm", 136 * n + 8, 136 * n + 136), V("z32", 0, 128), pat, base, 1)
+
+        def lay(buf, c0, w, src, rs, pat, base, fill):
+            st = rs[1] - rs[0]
+            if all(rs[p] == rs[0] + st * p for p in range(4)):
+                o = V(buf, c0, c0 + 4 * w)
+                mark(o, V(src, 0, 4 * w) if src else o, pat + [[-16 * st, 4]], base - 16 * rs[0], fill)
+            else:
+                for p in range(4):
+                    o = V(buf, c0 + p, c0 + 4 * w, 4)
+                    mark(o, V(src, 0, w) if src else o, pat, base - 16 * rs[p], fill)
+        pa, pb = [[-1, 8], [0, 8]], [[0, 8], [-1, 8]]
+        lay("D2", 256 * n, 64, "zb", ra, pa, 0, 128)
+        lay("D2", 256 * n, 64, None, ra, pa, -8, 1)
+        lay("D2", 256 * n, 64, None, rb, pb, 0, -128)
+        lay("D2", 256 * n, 64, None, rb, pb, -8, -1)
+        lay("KD", 512 * n, 64, "z32", ra, pa, 0, 1)
+        for s, rs in enumerate((ra, rb)):
+            lay("KD", 512 * n + 256 + 128 * s, 32, "z32", rs, [[0, 4], [-1, 8]], 0, 1)
+        lay("KD", 512 * n, 64, None, rb, pb, 0, -1)
+        for base in (-1, 7):
+            for s, rs in enumerate((ra, rb)):
+                lay("KD", 512 * n + 256 + 128 * s, 32, None, rs, [[-1, 4], [-1, 8]], base, -1)
+
+    DGp = lambda n, k: V("DGp", 384 * n + 128 * k, 384 * n + 128 * k + 128)
+    KD = lambda buf, n, p: V(buf, 512 * n + p, 512 * n + 512, 4)
+    D2 = lambda n, h: V("D2", 256 * n + h, 256 * n + 256, 2)
+
+    def maps_a(n):
+        act(DGp(n, 0), V("Perm", 136 * n, 136 * n + 128), scale=col("mlo"))
+        act(DGp(n, 1), V("Perm", 136 * n + 8, 136 * n + 136), scale=col("mhi"))
+        act(DGp(n, 2), V("Perm", 136 * n + 8, 136 * n + 136), scale=-1.0)
+
+    def maps_b(n, bank):
+        for h in range(2):
+            mm(B(bank, 128 * h, 128 * h + 128), D2(n, h), WW("01"[min(n, 1)], 2))
+        act(V("CM", 256 * n, 256 * n + 256), B(bank, 0, 256))
+
+    def maps_c(n):
+        act(V("KDb"), V("KD", 512 * n, 512 * n + 512))
+
+    def maps_d(n, bank):
+        for p in range(4):
+            mms(B(bank, 128 * p, 128 * p + 128), [(KD("KDb", 0, p), OH), (KD("KDb", 0, p), DGp(n, 0))])
+        act(V("KC", 512 * n, 512 * n + 512), V("KD", 512 * n, 512 * n + 512), scale=col("be" + "01"[min(n, 1)]))
+        act(V("RM", 512 * n, 512 * n + 512), B(bank), scale=col("w4"))
+
+    for n in range(3):
+        maps(n)
+
+    def table(n, chunks):
+        by_dma = {(ch, b) for k, (k0, bs) in DMAB.items() for ch in range(k0, k + 1) for b in bs}
+        jobs = [(ch, b) for ch in range(4) for b in range(1, 8) if (b not in DMA0 if n == 0 else (ch, b) not in by_dma)]
+        first = len(jobs) - 2 * NV[n] + min(n, 1)
+        for k, (ch, b) in enumerate(jobs):
+            if ch not in chunks:
+                continue
+            mm(B(k % 6), V("IW", 16 * b, 16 * b + 128), V("TT", 512 * ch, 512 * ch + 512))
+            o = V("TT", 2048 * b + 512 * ch, 2048 * b + 512 * ch + 512)
+            if k >= first and (k - first) % 2 == 0:
+                cp(o, B(k % 6))
+            else:
+                act(o, B(k % 6))
+
+    def offsets(src):
+        ts(V("t1"), src, col("rot"), A.add)
+        ts(V("t2"), V("t1"), 16383, A.bitwise_and)
+        cp(V("offU"), V("t2"))
+
+    maps_a(0)
+    maps_b(0, 7)
+    ts(V("t4"), V("SL"), 7, A.arith_shift_right)
+    ts(V("t3"), V("SL"), 127, A.bitwise_and)
+    cp(V("dh"), V("t4")); cp(V("dl"), V("t3"))
+    offsets(V("SL"))
+    cp(V("prU"), V("PR"))
+    mms(B(6, 0, 128), [(OH, V("dh")), (S1, V("dl"))])
+    mms(B(6, 128, 256), [(OL, V("dh")), (L1, V("dl"))])
+    act(V("IDd", 0, 256, 2), B(6, 0, 128))
+    act(V("IDd", 1, 256, 2), B(6, 128, 256))
+    table(0, range(4))
+    TW = V("TT")
+    ends = [sum(OUTW[:k + 1]) for k in range(len(OUTW))]
+    BW = lambda s, a: V(s, 15 - a, 143 - a)
+    row = lambda r: B(r // 2, 256 * (r % 2), 256 * (r % 2) + 256)
+    for n in range(3):
+        y = "01"[min(n, 1)]
+        for h in range(2):
+            cp(V("X", 512 * h, 512 * h + 512), I(TW, V("offU", 32 * h, 32 * h + 32)))
+            act(V("X", 1024 + 512 * h, 1536 + 512 * h), I(TW, V("offU", 64 + 32 * h, 96 + 32 * h)))
+        for k in range(4):
+            mm(B(k), V("on16", p1=1), V("prow16", p1=1), True, False)
+        for h in (0, 2, 1, 3):
+            mms(B(4, 64 * h, 64 * h + 64), [(V("I8"), V("X", 512 * h + j, 512 * h + 512, 8)) for j in range(8)])
+        cp(V("C16"), B(4, 0, 256))
+        for k in range(2):
+            mms(B(5, 8 * k, 8 * k + 8), [(V("prow16", 128 * k, 128 * k + 128, p1=1), V("on16", 0, 8, p1=1)),
+                                         (V("C16", 128 * k, 128 * k + 128), V("G8h"))])
+        for r in (4, 5, 2, 3, 6, 7, 0, 1):
+            mm(row(r), V("KR", 128 * r, 128 * r + 128), V("C16"), False, r % 2 == 1)
+        ts(V("neg"), B(5, 0, 16), -1.0, A.mult)
+        tt(V("Z"), B(4, 0, 256), V("trow"), A.add)
+        for r, k in ((2, 0), (2, 1), (0, 0), (1, 0), (0, 1), (1, 1)):
+            ts(M(16 * k, 16 * k + 16, r, r + 1), row(r), V("neg", 8 * k + r, 8 * k + r + 1), A.add, 0.0, A.is_gt)
+        for k in range(2):
+            for r in (4, 5, 6, 7, 3):
+                act(M(16 * k, 16 * k + 16, r, r + 1), row(r), F.Sign, bias=V("neg", 8 * k + r, 8 * k + r + 1))
+        m1 = lambda j: tt(V("M1", 256 * j, 256 * j + 256), V("X", j, 2048, 8), B(4, 0, 256), A.max)
+        for j in range(5):
+            m1(j)
+        mm(B(5, 16, 32), V("on16", p1=1), V("zrow", p1=1), True, False)
+        for k in range(2):
+            for b in range(16):
+                mm(B(5, 16 + b, 17 + b), M(16 * k + b, 16 * k + b + 1, 0, 8), V("onb", 0, 1), False, k + b == 16)
+        ts(V("posU"), B(5, 16, 32), col("psc"), A.mult, col("pbi"), A.add)
+        cp(I(V("Zs"), V("posU")), V("Z"))
+        ts(V("od"), V("Zs"), 256 * MAGIC, A.add, -256 * MAGIC, A.add)
+        for j in range(5, 8):
+            m1(j)
+        if n == 0:
+            maps_c(0)
+            maps_d(0, 6)
+        for j in range(8):
+            mm(row(j), I0, V("X", j, 2048, 8))
+        mms(B(7, 0, 256), [(V("Perm", 136 * n + 8, 136 * n + 136), V("Zs")), (DGp(n, 2), V("od"))])
+        act(V("Cps"), B(7, 0, 256), bias=127.875)
+        mms(B(5, 32, 48), [(BW("BWb", a), V("od", a, 256, 16)) for a in range(16)])
+        cp(V("Cp"), I(V("Cps"), V("posU")))
+        ts(V("ordU"), B(5, 32, 48), 1.0 / 4096, A.mult)
+        act(V("IDs"), I(V("IDd"), V("ordU")))
+        mms(B(6, 0, 256), [(BW("BWp", j), V("M1", 256 * j, 256 * j + 256)) for j in range(4)], stop=False)
+        for h in range(2):
+            mm(B(4, 256 * h, 256 * h + 256), D2(n, h), V("IDs"))
+        mms(B(6, 0, 256), [(BW("BWp", j), V("M1", 256 * j, 256 * j + 256)) for j in range(4, 8)], start=False, stop=False)
+        act(V("AB"), B(4), F.Abs)
+        act(V("Eq"), V("AB"), F.Relu, bias=1.0, scale=-1.0)
+        for j in range(8):
+            tt(V("M2", 256 * j, 256 * j + 256), row(j), V("Cp"), A.max)
+        for j in range(8):
+            mm(B(6, 0, 256), BW("BWn", j), V("M2", 256 * j, 256 * j + 256), False, j == 7)
+            if j == 6:
+                mms(B(7, 0, 256), [(V("CM", 256 * n + 128 * h, 256 * n + 128 * h + 128), V("Eq", 256 * h, 256 * h + 256)) for h in range(2)])
+                act(V("com"), B(7, 0, 256), bias=col("m8"))
+        if n < 2:
+            maps_a(n + 1)
+            maps_c(n + 1)
+        ts(V("Kf"), B(6, 0, 256), col("sig" + y), A.mult, col("q" + y), A.add)
+        cp(V("Ks"), I(V("Kf"), V("ordU")))
+        for p in range(4):
+            mm(B(p, 0, 256), KD("KC", n, p), V("com"), True, False)
+        sg = lambda p: V("sg", 256 * p, 256 * p + 256)
+        rk = lambda p: mm(B(5, 0, 256), V("RM", 512 * n + 128 * p, 512 * n + 128 * p + 128), sg(p), p == 0, p == 3)
+        vw = lambda bank, own, k: mms(B(bank, 0, 256), [(own, V("IDs")), (DGp(n, k), V("IDs")), (WW(y, 0), V("com")), (WW(y, 1), V("com"))])
+        for p in range(4):
+            mm(B(p, 0, 256), KD("KD", n, p), V("Ks"), False, True)
+            if p % 2 == 0:
+                act(sg(p), B(p, 0, 256), F.Sign)
+            else:
+                ts(sg(p), B(p, 0, 256), -1.0, A.max, 1.0, A.min)
+        for p in range(4):
+            rk(p)
+        vw(7, OH, 0)
+        vw(4, OL, 1)
+        ts(V("Tq"), B(5, 0, 256), 64.0, A.is_ge, col("cA" + y), A.mult)
+        tt(V("Rq"), B(5, 0, 256), V("Tq"), A.add)
+        tt(V("vv", 0, 256), B(7, 0, 256), V("Rq"), A.add)
+        tt(V("vv", 256, 512), B(4, 0, 256), V("Rq"), A.add)
+        if n < 2:
+            maps_b(n + 1, 0)
+            maps_d(n + 1, 1)
+        for j in range(8):
+            ts(V("FF", 512 * j, 512 * j + 512), V("vv"), 128.0 * j, A.max, 128.0 * j + 128, A.min)
+            for k in range(2):
+                mm(B(6, 0, 256), BW("BWp", 8 * k + j), V("FF", 512 * j + 256 * k, 512 * j + 256 * k + 256), j + k == 0, j + k == 8)
+        ts(V("Ns"), B(6, 0, 256), col("nb" + y), A.add)
+        cp(V("IDd"), I(V("Ns"), V("posU")))
+        ev, od = V("IDd", 0, 256, 2), V("IDd", 1, 256, 2)
+        mms(B(5, 0, 128), [(H0, ev), (OL, ev), (H1, od), (L1, od)])
+        offsets(B(5, 0, 128))
+        if n == 2:
+            act(V("YL"), B(5, 0, 128))
+            dma("Y", D("stl"), V("YL"), "dl")
+            dma("Y", D("ldl", me, me + 1), V("YL", p0=r0, p1=r1), "dlo")
+            send([("stl", "ldl")], "ayl")
+        ts(V("Xn", 0, 1024), I(TW, V("offU", 0, 64)), 2048.5, A.add)
+        act(V("Xn", 1024, 2048), I(TW, V("offU", 64, 128)), bias=2048.5)
+        xh = lambda ch: V("XH", 256 * ch - 256, 256 * ch + 256)
+        for ch in (1, 3):
+            act(xh(ch), I(V("Xn"), V("prU", 32 * ch, 32 * ch + 32)), bias=-2048.5)
+        for ch in range(4):
+            c0, c1 = 512 * ch, 512 * ch + 512
+            if ch % 2 == 0:
+                mms(B(6 + ch // 2), [(V("on16", p1=1), V("qrow", p1=1)), (V("Ih"), V("TT", c1, c1 + 512)), (V("Ih"), xh(ch + 1))])
+                tt(V("N16", c0, c1), I(V("Xn"), V("prU", 32 * ch, 32 * ch + 32)), V("TT", c0, c1), A.add)
+                ts(V("TT", c0, c1), V("N16", c0, c1), -2048.0, A.add, 0.5, A.mult)
+            else:
+                ts(V("TT", c0, c1), B(6 + ch // 2), MAGIC, A.add, -MAGIC, A.add)
+            if n < 2 and ch in DMAB:
+                k0, bs = DMAB[ch]
+                for b in bs:
+                    s, o = 16 * b, 2048 * b
+                    dma("Y", V("TT", o + 512 * k0, o + c1, p1=128 - s), V("TT", 512 * k0, c1, p0=s), "dT%d" % (n + 1))
+                    dma("Y", V("TT", o + 512 * k0, o + c1, p0=128 - s), V("TT", 512 * k0, c1, p1=s), "dT%d" % (n + 1))
+            if n < 2 and ch == 1:
+                table(n + 1, (0,))
+            if n == 2 and c1 in ends:
+                k = ends.index(c1)
+                dma("Y", D("sto%d" % k), V("TT", c1 - OUTW[k], c1), "do%d" % k)
+                dma("S", D("ldo%d" % k, me, me + 1), V("TT", c1 - OUTW[k], c1, p0=r0, p1=r1), "doo%d" % k)
+                send([("sto%d" % k, "ldo%d" % k)], "ao%d" % k)
+        if n < 2:
+            table(n + 1, (1, 2, 3))
+    dma("Y", E("yl"), D("ldl"), "dyl")
+    for k in range(len(OUTW)):
+        dma("G", E("yx", 0, 128, ends[k] - OUTW[k], ends[k]), D("ldo%d" % k), "dy%d" % k)
+
+    hist = {}
+    for n, o in enumerate(ops):
+        deps = set()
+        for a, w in [(a, True) for a in o["wr"]] + [(a, False) for a in o["rd"]]:
+            bank = SCRATCH[a[1]][0] == "psum"
+            for m, b, w2 in hist.get(a[1], []):
+                q2 = ops[m]["q"]
+                if q2 == "P" and o["q"] == "P":
+                    continue
+                if (bank and q2 != o["q"]) or ((w or w2) and meet(a, b)):
+                    deps.add(m)
+        for a in o["wr"]:
+            hist.setdefault(a[1], []).append((n, a, True))
+        for a in o["rd"]:
+            hist.setdefault(a[1], []).append((n, a, False))
+        last = {}
+        for m in deps:
+            key = ops[m]["sem"] or ops[m]["q"]
+            last[key] = max(last.get(key, -1), m)
+        o["deps"] = sorted(last.values())
+    seen = {}
+    for n, o in enumerate(ops):
+        keep = []
+        for m in o["deps"]:
+            key = (o["q"], ops[m]["sem"] or ops[m]["q"])
+            if seen.get(key, -1) < m:
+                seen[key] = m
+                keep.append(m)
+                ops[m]["need"] = True
+        o["deps"] = keep
+    total = {}
+    for o in ops:
+        if o["sem"]:
+            total[o["sem"]] = total.get(o["sem"], 0) + o["inc"]
+        elif o.get("need"):
+            total["c" + o["q"]] = o["cnt"] = total.get("c" + o["q"], 0) + 1
+    eng = {"V": g.vector, "S": g.scalar, "P": g.tensor, "G": g, "Y": g.sync}
+    waited = {}
+    for o in ops:
+        if o["q"] == "R":
+            continue
+        for m in o["deps"]:
+            s = ops[m]["sem"] or "c" + ops[m]["q"]
+            v = total[s] if ops[m]["sem"] else ops[m]["cnt"]
+            if waited.get((o["q"], s), 0) < v:
+                eng[o["q"]].wait_ge(T.sem[s], v)
+                waited[(o["q"], s)] = v
+        h = o["fn"]()
+        if o.get("remote"):
+            continue
+        if o["sem"]:
+            h.then_inc(T.sem[o["sem"]], 16)
+        elif o.get("need"):
+            h.then_inc(T.sem["c" + o["q"]], 1)
+    for s, v in total.items():
+        if max([waited.get((q, s), 0) for q in eng]) < v:
+            g.wait_ge(T.sem[s], v)

@@ -4,13 +4,14 @@ from concourse.mybir import AluOpType as A, ActivationFunctionType as F
 DS = (1, 6, 4)
 OUTW = (1024, 512, 512)
 DMA0 = (5, 6, 7)
-DMAB = {1: (0, (5, 6, 7)), 2: (2, (5, 6, 7))}
-NV = (8, 8, 8)
+DMAB = {1: (0, (3, 4, 5, 6, 7)), 2: (2, (5, 6, 7))}
+NV = (0, 4, 4)
 MAGIC = 12582912.0
 f32, bf, f16, i32, u16 = "float32", "bfloat16", "float16", "int32", "uint16"
 
 SCRATCH = {
-    "stx": ("dram", [8, 128, 256], bf), "ldx": ("dram", [8, 128, 256], bf),
+    "stx0": ("dram", [8, 128, 128], bf), "ldx0": ("dram", [8, 128, 128], bf),
+    "stx1": ("dram", [8, 128, 128], bf), "ldx1": ("dram", [8, 128, 128], bf),
     "sts": ("dram", [8, 128, 16], i32), "lds": ("dram", [8, 128, 16], i32),
     "stp": ("dram", [8, 128, 16], i32), "ldp": ("dram", [8, 128, 16], i32),
     "stl": ("dram", [8, 128, 16], f32), "ldl": ("dram", [8, 128, 16], f32),
@@ -25,12 +26,12 @@ for _n, _w, _d in (
     ("TT", 16384, bf), ("X", 2048, bf), ("Xn", 2048, f32), ("N16", 2048, f16), ("M1", 2048, f16), ("M2", 2048, f16),
     ("FF", 4096, f16), ("SL", 128, i32), ("PR", 128, i32), ("prU", 128, u16), ("offU", 128, u16),
     ("t1", 128, i32), ("t2", 128, i32), ("t3", 128, i32), ("t4", 128, i32), ("dh", 128, bf), ("dl", 128, bf),
-    ("IDd", 256, bf), ("IDs", 256, bf), ("Z", 256, f32), ("C16", 256, f16), ("Zs", 256, f32), ("od", 256, bf),
+    ("IDd", 256, bf), ("wr", 256, bf), ("IDs", 256, bf), ("Z", 256, f32), ("C16", 256, f16), ("Zs", 256, f32), ("od", 256, bf),
     ("Cps", 256, f32), ("Cp", 256, f32), ("neg", 16, f32), ("posU", 16, u16), ("ordU", 16, u16),
     ("Kf", 256, f32), ("Ks", 256, f32), ("AB", 512, f32), ("Eq", 512, bf), ("com", 256, bf),
     ("sg", 1024, bf), ("Tq", 256, f32), ("Rq", 256, f32), ("vv", 512, f16), ("Ns", 256, bf), ("YL", 128, f32),
     ("i256", 256, f32), ("i144", 144, f32), ("cgrp", 128, f32), ("prow", 256, f32), ("trow", 256, f32), ("prow16", 512, f16),
-    ("qrow", 512, f16), ("zrow", 16, f16), ("XH", 1024, bf), ("Ih", 128, bf),
+    ("qrow", 512, f16), ("zrow", 16, f16), ("XH", 2048, bf), ("Ih", 128, bf),
     ("pi", 8, i32), ("pj", 8, i32), ("cols", 64, f32),
     ("IW", 256, bf), ("I8", 128, bf), ("BWp", 144, f16), ("BWn", 144, f16), ("BWb", 144, bf), ("blk", 128, bf), ("KR", 1024, f16),
     ("G8", 8, f32), ("G8h", 8, f16), ("on16", 128, f16), ("onb", 8, bf), ("z32", 256, f32), ("zb", 256, bf),
@@ -39,8 +40,9 @@ for _n, _w, _d in (
 ):
     SCRATCH[_n] = ("sbuf", [128, _w], _d)
 
-SEMAPHORES = ["cV", "cS", "cP", "cG", "sent", "ax", "al", "ayl", "dx", "dxo", "ds", "dso", "dp", "dpo", "dt0", "dsl", "dpr",
-              "dT0", "dT1", "dT2", "dl", "dlo", "dyl"] + ["%s%d" % (a, k) for a in ("ao", "do", "doo", "dy") for k in range(len(OUTW))]
+SEMAPHORES = ["cV", "cS", "cP", "cG", "sent", "ax0", "ax1", "al", "ayl", "dx0", "dx1", "dxo0", "dxo1", "ds", "dso", "dp", "dpo",
+              "dt0", "dt1", "dsl", "dpr", "dT0", "dT1", "dT2", "dl", "dlo", "dyl"] + [
+                  "%s%d" % (a, k) for a in ("ao", "do", "doo", "dy") for k in range(len(OUTW))]
 
 
 def V(name, c0=0, c1=None, st=1, p0=0, p1=128):
@@ -173,10 +175,12 @@ def rank_program(g, core, T, topo):
         return V("cols", cnames[n], cnames[n] + 1)
 
     r0, r1 = 16 * me, 16 * me + 16
-    dma("Y", D("stx"), E("x"), "dx")
+    for h in range(2):
+        dma("Y", D("stx%d" % h), E("x", 0, 128, 1024 * h, 1024 * h + 1024), "dx%d" % h)
     dma("S", D("sts"), E("sl"), "ds")
     dma("G", D("stp"), E("prey"), "dp")
-    dma("Y", D("ldx", me, me + 1), E("x", r0, r1), "dxo")
+    for h in range(2):
+        dma("Y", D("ldx%d" % h, me, me + 1), E("x", r0, r1, 1024 * h, 1024 * h + 1024), "dxo%d" % h)
     dma("S", D("lds", me, me + 1), E("sl", r0, r1), "dso")
     dma("S", D("ldp", me, me + 1), E("prey", r0, r1), "dpo")
     iota(V("pi", 0, 1), [[0, 1]], 0, 1, False)
@@ -184,14 +188,18 @@ def rank_program(g, core, T, topo):
     iota(V("i144"), [[1, 144]])
     iota(V("cgrp"), [[1, 8], [0, 16]])
     send([("sts", "lds"), ("stp", "ldp")], "al")
-    send([("stx", "ldx")], "ax")
+    send([("stx0", "ldx0")], "ax0")
+    send([("stx1", "ldx1")], "ax1")
     iota(V("prow"), [[1, 256]])
     dma("Y", V("SL"), D("lds"), "dsl")
     dma("Y", V("PR"), D("ldp"), "dpr")
-    dma("Y", V("TT", 0, 2048), D("ldx"), "dt0")
-    for b in DMA0:
-        dma("Y", V("TT", 2048 * b, 2048 * b + 2048, p1=128 - 16 * b), D("ldx", b, 8), "dT0")
-        dma("Y", V("TT", 2048 * b, 2048 * b + 2048, p0=128 - 16 * b), D("ldx", 0, b), "dT0")
+    for h in range(2):
+        dma("Y", V("TT", 1024 * h, 1024 * h + 1024), D("ldx%d" % h), "dt%d" % h)
+    for h in range(2):
+        for b in DMA0:
+            o = 2048 * b + 1024 * h
+            dma("Y", V("TT", o, o + 1024, p1=128 - 16 * b), D("ldx%d" % h, b, 8), "dT0")
+            dma("Y", V("TT", o, o + 1024, p0=128 - 16 * b), D("ldx%d" % h, 0, b), "dT0")
 
     ms(V("z32"), 0.0); ms(V("zb"), 0.0); ms(V("on16"), 1.0); ms(V("onb"), 1.0)
     for n in range(3):
@@ -216,12 +224,14 @@ def rank_program(g, core, T, topo):
     ts(col("mlo128"), col("i"), 8.0, A.is_lt, 128.0, A.mult)
     ts(col("rot"), col("grp"), -2048.0, A.mult, 16384.0, A.add)
     ts(col("g15"), col("grp"), 16.0, A.mult, 15.0, A.add)
-    ts(col("psc"), col("grp"), 2.5, A.is_lt, 0.5, A.mult)
-    ts(col("pbi"), col("grp"), 2.5, A.is_gt, 127.5, A.mult)
+    ts(col("psc"), col("grp"), 3.5, A.is_lt, 0.5, A.mult)
+    ts(col("pbi"), col("grp"), 3.5, A.is_gt, 127.5, A.mult)
     ts(col("w4"), col("p31"), 24.0, A.is_ge, col("sd1"), A.mult)
     ts(V("G8"), V("i144", 0, 8), col("grp"), A.is_equal, -2048.0, A.mult)
     ts(V("blk"), V("cgrp"), col("grp"), A.is_equal)
     ts(col("psc"), col("psc"), 0.5, A.add)
+    ts(col("thr"), col("g15"), -15.0, A.add, col("mlo"), A.mult)
+    ts(col("rot0"), col("grp"), -2048.0, A.mult)
     ts(col("w4"), col("w4"), -32.0, A.mult, 64.0, A.add)
     ts(V("BWp"), V("i144"), col("g15"), A.is_equal)
     ts(V("BWb"), V("i144"), col("g15"), A.is_equal)
@@ -236,7 +246,9 @@ def rank_program(g, core, T, topo):
     act(V("Ih"), I0, scale=0.5)
     for o, a, c in ((OH, I0, "mlo"), (OL, Iup, "mhi"), (S1, Idn, "mlo"), (L1, I0, "mhi"), (H0, I0, "mlo128"), (H1, Idn, "mlo128")):
         act(o, a, scale=col(c))
-    for y in "01":
+    WW = lambda y, k: V("WW", 384 * int(y) + 128 * k, 384 * int(y) + 128 * k + 128)
+
+    def side(y):
         sd = col("sd" + y)
         ts(col("sig" + y), sd, -256.0, A.mult, 128.0, A.add)
         ts(col("q" + y), sd, 8.0, A.mult, col("j"), A.add)
@@ -251,11 +263,14 @@ def rank_program(g, core, T, topo):
         ts(col("nb" + y), sd, 1024.0, A.mult, col("nb" + y), A.add)
         ts(col("be" + y), col("be" + y), 8192.0, A.mult)
         ts(col("s2" + y), col("s1" + y), -0.125, A.mult, col("s3" + y), A.add)
-    WW = lambda y, k: V("WW", 384 * int(y) + 128 * k, 384 * int(y) + 128 * k + 128)
-    for y in "01":
+
+    def side_maps(y):
+        act(WW(y, 2), I0, scale=col("de" + y))
         act(WW(y, 0), I0, scale=col("s1" + y))
         act(WW(y, 1), V("blk"), scale=col("s2" + y))
-        act(WW(y, 2), I0, scale=col("de" + y))
+
+    side("0")
+    side_maps("0")
     cp(V("prow16", 0, 256, p1=1), V("prow", p1=1))
     cp(V("prow16", 256, 512, p1=1), V("prow", p1=1))
     ts(V("trow"), V("prow"), 256.0, A.mult, -127.875, A.add)
@@ -325,33 +340,22 @@ def rank_program(g, core, T, topo):
     def table(n, chunks):
         by_dma = {(ch, b) for k, (k0, bs) in DMAB.items() for ch in range(k0, k + 1) for b in bs}
         jobs = [(ch, b) for ch in range(4) for b in range(1, 8) if (b not in DMA0 if n == 0 else (ch, b) not in by_dma)]
-        first = len(jobs) - 2 * NV[n] + min(n, 1)
         for k, (ch, b) in enumerate(jobs):
             if ch not in chunks:
                 continue
             mm(B(k % 6), V("IW", 16 * b, 16 * b + 128), V("TT", 512 * ch, 512 * ch + 512))
             o = V("TT", 2048 * b + 512 * ch, 2048 * b + 512 * ch + 512)
-            if k >= first and (k - first) % 2 == 0:
+            if k >= NV[n] and (k - NV[n]) % 2 == 0:
                 cp(o, B(k % 6))
             else:
                 act(o, B(k % 6))
 
-    def offsets(src):
-        ts(V("t1"), src, col("rot"), A.add)
-        ts(V("t2"), V("t1"), 16383, A.bitwise_and)
-        cp(V("offU"), V("t2"))
-
     maps_a(0)
-    maps_b(0, 7)
+    ts(V("t1"), V("SL"), col("rot"), A.add)
     ts(V("t4"), V("SL"), 7, A.arith_shift_right)
+    ts(V("t2"), V("t1"), 16383, A.bitwise_and)
     ts(V("t3"), V("SL"), 127, A.bitwise_and)
-    cp(V("dh"), V("t4")); cp(V("dl"), V("t3"))
-    offsets(V("SL"))
-    cp(V("prU"), V("PR"))
-    mms(B(6, 0, 128), [(OH, V("dh")), (S1, V("dl"))])
-    mms(B(6, 128, 256), [(OL, V("dh")), (L1, V("dl"))])
-    act(V("IDd", 0, 256, 2), B(6, 0, 128))
-    act(V("IDd", 1, 256, 2), B(6, 128, 256))
+    cp(V("offU"), V("t2"))
     table(0, range(4))
     TW = V("TT")
     ends = [sum(OUTW[:k + 1]) for k in range(len(OUTW))]
@@ -362,6 +366,8 @@ def rank_program(g, core, T, topo):
         for h in range(2):
             cp(V("X", 512 * h, 512 * h + 512), I(TW, V("offU", 32 * h, 32 * h + 32)))
             act(V("X", 1024 + 512 * h, 1536 + 512 * h), I(TW, V("offU", 64 + 32 * h, 96 + 32 * h)))
+        if n == 0:
+            cp(V("dh"), V("t4")); cp(V("dl"), V("t3")); cp(V("prU"), V("PR"))
         for k in range(4):
             mm(B(k), V("on16", p1=1), V("prow16", p1=1), True, False)
         for h in (0, 2, 1, 3):
@@ -370,17 +376,21 @@ def rank_program(g, core, T, topo):
         for k in range(2):
             mms(B(5, 8 * k, 8 * k + 8), [(V("prow16", 128 * k, 128 * k + 128, p1=1), V("on16", 0, 8, p1=1)),
                                          (V("C16", 128 * k, 128 * k + 128), V("G8h"))])
-        for r in (4, 5, 2, 3, 6, 7, 0, 1):
+        for r in (4, 5, 0, 1, 6, 7, 2, 3):
             mm(row(r), V("KR", 128 * r, 128 * r + 128), V("C16"), False, r % 2 == 1)
-        ts(V("neg"), B(5, 0, 16), -1.0, A.mult)
+        if n == 0:
+            mms(B(6, 0, 128), [(OH, V("dh")), (S1, V("dl"))])
+            mms(B(6, 128, 256), [(OL, V("dh")), (L1, V("dl"))])
+        act(V("neg"), B(5, 0, 16), scale=-1.0)
         tt(V("Z"), B(4, 0, 256), V("trow"), A.add)
-        for r, k in ((2, 0), (2, 1), (0, 0), (1, 0), (0, 1), (1, 1)):
-            ts(M(16 * k, 16 * k + 16, r, r + 1), row(r), V("neg", 8 * k + r, 8 * k + r + 1), A.add, 0.0, A.is_gt)
         for k in range(2):
-            for r in (4, 5, 6, 7, 3):
+            for r in range(4):
+                ts(M(16 * k, 16 * k + 16, r, r + 1), row(r), V("neg", 8 * k + r, 8 * k + r + 1), A.add, 0.0, A.is_gt)
+        for k in range(2):
+            for r in range(4, 8):
                 act(M(16 * k, 16 * k + 16, r, r + 1), row(r), F.Sign, bias=V("neg", 8 * k + r, 8 * k + r + 1))
         m1 = lambda j: tt(V("M1", 256 * j, 256 * j + 256), V("X", j, 2048, 8), B(4, 0, 256), A.max)
-        for j in range(5):
+        for j in range(3):
             m1(j)
         mm(B(5, 16, 32), V("on16", p1=1), V("zrow", p1=1), True, False)
         for k in range(2):
@@ -389,17 +399,19 @@ def rank_program(g, core, T, topo):
         ts(V("posU"), B(5, 16, 32), col("psc"), A.mult, col("pbi"), A.add)
         cp(I(V("Zs"), V("posU")), V("Z"))
         ts(V("od"), V("Zs"), 256 * MAGIC, A.add, -256 * MAGIC, A.add)
-        for j in range(5, 8):
+        for j in range(3, 8):
             m1(j)
         if n == 0:
+            act(V("IDd", 0, 256, 2), B(6, 0, 128))
+            act(V("IDd", 1, 256, 2), B(6, 128, 256))
             maps_c(0)
-            maps_d(0, 6)
+            maps_b(0, 7)
         for j in range(8):
             mm(row(j), I0, V("X", j, 2048, 8))
         mms(B(7, 0, 256), [(V("Perm", 136 * n + 8, 136 * n + 136), V("Zs")), (DGp(n, 2), V("od"))])
         act(V("Cps"), B(7, 0, 256), bias=127.875)
+        act(V("Cp"), I(V("Cps"), V("posU")))
         mms(B(5, 32, 48), [(BW("BWb", a), V("od", a, 256, 16)) for a in range(16)])
-        cp(V("Cp"), I(V("Cps"), V("posU")))
         ts(V("ordU"), B(5, 32, 48), 1.0 / 4096, A.mult)
         act(V("IDs"), I(V("IDd"), V("ordU")))
         mms(B(6, 0, 256), [(BW("BWp", j), V("M1", 256 * j, 256 * j + 256)) for j in range(4)], stop=False)
@@ -415,11 +427,12 @@ def rank_program(g, core, T, topo):
             if j == 6:
                 mms(B(7, 0, 256), [(V("CM", 256 * n + 128 * h, 256 * n + 128 * h + 128), V("Eq", 256 * h, 256 * h + 256)) for h in range(2)])
                 act(V("com"), B(7, 0, 256), bias=col("m8"))
-        if n < 2:
-            maps_a(n + 1)
-            maps_c(n + 1)
+        if n == 0:
+            maps_d(0, 4)
         ts(V("Kf"), B(6, 0, 256), col("sig" + y), A.mult, col("q" + y), A.add)
         cp(V("Ks"), I(V("Kf"), V("ordU")))
+        if n == 0:
+            side("1")
         for p in range(4):
             mm(B(p, 0, 256), KD("KC", n, p), V("com"), True, False)
         sg = lambda p: V("sg", 256 * p, 256 * p + 256)
@@ -439,36 +452,47 @@ def rank_program(g, core, T, topo):
         tt(V("Rq"), B(5, 0, 256), V("Tq"), A.add)
         tt(V("vv", 0, 256), B(7, 0, 256), V("Rq"), A.add)
         tt(V("vv", 256, 512), B(4, 0, 256), V("Rq"), A.add)
+        if n == 0:
+            side_maps("1")
         if n < 2:
-            maps_b(n + 1, 0)
-            maps_d(n + 1, 1)
+            maps_a(n + 1)
+            maps_c(n + 1)
         for j in range(8):
             ts(V("FF", 512 * j, 512 * j + 512), V("vv"), 128.0 * j, A.max, 128.0 * j + 128, A.min)
             for k in range(2):
                 mm(B(6, 0, 256), BW("BWp", 8 * k + j), V("FF", 512 * j + 256 * k, 512 * j + 256 * k + 256), j + k == 0, j + k == 8)
+        if n < 2:
+            maps_b(n + 1, 0)
+            maps_d(n + 1, 1)
         ts(V("Ns"), B(6, 0, 256), col("nb" + y), A.add)
         cp(V("IDd"), I(V("Ns"), V("posU")))
         ev, od = V("IDd", 0, 256, 2), V("IDd", 1, 256, 2)
-        mms(B(5, 0, 128), [(H0, ev), (OL, ev), (H1, od), (L1, od)])
-        offsets(B(5, 0, 128))
+        ts(V("wr"), V("IDd"), col("thr"), A.is_lt, 128.0, A.mult)
+        ids = [(H0, ev), (OL, ev), (H1, od), (L1, od)]
+        mms(B(5, 0, 128), ids + [(H0, V("wr", 0, 256, 2)), (H1, V("wr", 1, 256, 2))])
+        ts(V("offU"), B(5, 0, 128), col("rot0"), A.add)
         if n == 2:
-            act(V("YL"), B(5, 0, 128))
+            mms(B(4, 0, 128), ids)
+            act(V("YL"), B(4, 0, 128))
             dma("Y", D("stl"), V("YL"), "dl")
             dma("Y", D("ldl", me, me + 1), V("YL", p0=r0, p1=r1), "dlo")
             send([("stl", "ldl")], "ayl")
         ts(V("Xn", 0, 1024), I(TW, V("offU", 0, 64)), 2048.5, A.add)
         act(V("Xn", 1024, 2048), I(TW, V("offU", 64, 128)), bias=2048.5)
-        xh = lambda ch: V("XH", 256 * ch - 256, 256 * ch + 256)
-        for ch in (1, 3):
+        xh = lambda ch: V("XH", 512 * ch, 512 * ch + 512)
+        by_s = (1, 3) if n < 2 else (1, 2, 3)
+        bank = {1: 6, 2: 5, 3: 7}
+        for ch in by_s:
             act(xh(ch), I(V("Xn"), V("prU", 32 * ch, 32 * ch + 32)), bias=-2048.5)
         for ch in range(4):
             c0, c1 = 512 * ch, 512 * ch + 512
-            if ch % 2 == 0:
-                mms(B(6 + ch // 2), [(V("on16", p1=1), V("qrow", p1=1)), (V("Ih"), V("TT", c1, c1 + 512)), (V("Ih"), xh(ch + 1))])
+            if ch + 1 in by_s:
+                mms(B(bank[ch + 1]), [(V("on16", p1=1), V("qrow", p1=1)), (V("Ih"), V("TT", c1, c1 + 512)), (V("Ih"), xh(ch + 1))])
+            if ch not in by_s:
                 tt(V("N16", c0, c1), I(V("Xn"), V("prU", 32 * ch, 32 * ch + 32)), V("TT", c0, c1), A.add)
                 ts(V("TT", c0, c1), V("N16", c0, c1), -2048.0, A.add, 0.5, A.mult)
             else:
-                ts(V("TT", c0, c1), B(6 + ch // 2), MAGIC, A.add, -MAGIC, A.add)
+                ts(V("TT", c0, c1), B(bank[ch]), MAGIC, A.add, -MAGIC, A.add)
             if n < 2 and ch in DMAB:
                 k0, bs = DMAB[ch]
                 for b in bs:
@@ -476,14 +500,14 @@ def rank_program(g, core, T, topo):
                     dma("Y", V("TT", o + 512 * k0, o + c1, p1=128 - s), V("TT", 512 * k0, c1, p0=s), "dT%d" % (n + 1))
                     dma("Y", V("TT", o + 512 * k0, o + c1, p0=128 - s), V("TT", 512 * k0, c1, p1=s), "dT%d" % (n + 1))
             if n < 2 and ch == 1:
-                table(n + 1, (0,))
+                table(n + 1, (0, 1))
             if n == 2 and c1 in ends:
                 k = ends.index(c1)
                 dma("Y", D("sto%d" % k), V("TT", c1 - OUTW[k], c1), "do%d" % k)
-                dma("S", D("ldo%d" % k, me, me + 1), V("TT", c1 - OUTW[k], c1, p0=r0, p1=r1), "doo%d" % k)
+                dma("Y", D("ldo%d" % k, me, me + 1), V("TT", c1 - OUTW[k], c1, p0=r0, p1=r1), "doo%d" % k)
                 send([("sto%d" % k, "ldo%d" % k)], "ao%d" % k)
         if n < 2:
-            table(n + 1, (1, 2, 3))
+            table(n + 1, (2, 3))
     dma("Y", E("yl"), D("ldl"), "dyl")
     for k in range(len(OUTW)):
         dma("G", E("yx", 0, 128, ends[k] - OUTW[k], ends[k]), D("ldo%d" % k), "dy%d" % k)

from concourse.bass import DstId, RemoteDMATransfer
from concourse.mybir import AluOpType as A, ActivationFunctionType as F

DS = (1, 6, 4)
OUTW = (1024, 512, 512)
DMA0 = (5, 6, 7)
DMAB = {1: (0, (3, 4, 5, 6, 7)), 2: (2, (5, 6, 7))}
NV = (0, 4, 4)
MAGIC = 12582912.0
f32, bf, f16, i32, u16 = "float32", "bfloat16", "float16", "int32", "uint16"

SCRATCH = {
    "stx0": ("dram", [8, 128, 128], bf), "ldx0": ("dram", [8, 128, 128], bf),
    "stx1": ("dram", [8, 128, 128], bf), "ldx1": ("dram", [8, 128, 128], bf),
    "sts": ("dram", [8, 128, 16], i32), "lds": ("dram", [8, 128, 16], i32),
    "stp": ("dram", [8, 128, 16], i32), "ldp": ("dram", [8, 128, 16], i32),
    "stl": ("dram", [8, 128, 16], f32), "ldl": ("dram", [8, 128, 16], f32),
    "Mall": ("sbuf", [128, 32, 8, 16], bf),
}
for _k, _w in enumerate(OUTW):
    SCRATCH["sto%d" % _k] = ("dram", [8, 128, _w // 8], bf)
    SCRATCH["ldo%d" % _k] = ("dram", [8, 128, _w // 8], bf)
for _k in range(8):
    SCRATCH["B%d" % _k] = ("psum", [128, 512], f32)
for _n, _w, _d in (
    ("TT", 16384, bf), ("X", 2048, bf), ("Xn", 2048, f32), ("N16", 2048, f16), ("M1", 2048, f16), ("M2", 2048, f16),
    ("FF", 4096, f16), ("SL", 128, i32), ("PR", 128, i32), ("prU", 128, u16), ("offU", 128, u16),
    ("t1", 128, i32), ("t2", 128, i32), ("t3", 128, i32), ("t4", 128, i32), ("dh", 128, bf), ("dl", 128, bf),
    ("IDd", 256, bf), ("wr", 256, bf), ("IDs", 256, bf), ("Z", 256, f32), ("C16", 256, f16), ("Zs", 256, f32), ("od", 256, bf),
    ("Cps", 256, f32), ("Cp", 256, f32), ("neg", 16, f32), ("posU", 16, u16), ("ordU", 16, u16),
    ("Kf", 256, f32), ("Ks", 256, f32), ("AB", 512, f32), ("Eq", 512, bf), ("com", 256, bf),
    ("sg", 1024, bf), ("Tq", 256, f32), ("Rq", 256, f32), ("vv", 512, f16), ("Ns", 256, bf), ("YL", 128, f32),
    ("i256", 256, f32), ("i144", 144, f32), ("cgrp", 128, f32), ("prow", 256, f32), ("trow", 256, f32), ("prow16", 512, f16),
    ("qrow", 512, f16), ("zrow", 16, f16), ("XH", 2048, bf), ("Ih", 128, bf),
    ("pi", 8, i32), ("pj", 8, i32), ("cols", 64, f32),
    ("IW", 256, bf), ("I8", 128, bf), ("BWp", 144, f16), ("BWn", 144, f16), ("BWb", 144, bf), ("blk", 128, bf), ("KR", 1024, f16),
    ("G8", 8, f32), ("G8h", 8, f16), ("on16", 128, f16), ("onb", 8, bf), ("z32", 256, f32), ("zb", 256, bf),
    ("SM", 768, bf), ("WW", 768, bf), ("Perm", 408, f32), ("D2", 768, bf), ("KD", 1536, f32),
    ("DGp", 1152, bf), ("KDb", 512, bf), ("KC", 1536, bf), ("RM", 1536, bf), ("CM", 768, bf),
):
    SCRATCH[_n] = ("sbuf", [128, _w], _d)

SEMAPHORES = ["cV", "cS", "cP", "cG", "sent", "ax0", "ax1", "al", "ayl", "dx0", "dx1", "dxo0", "dxo1", "ds", "dso", "dp", "dpo",
              "dt0", "dt1", "dsl", "dpr", "dT0", "dT1", "dT2", "dl", "dlo", "dyl"] + [
                  "%s%d" % (a, k) for a in ("ao", "do", "doo", "dy") for k in range(len(OUTW))]


def V(name, c0=0, c1=None, st=1, p0=0, p1=128):
    return ("c", name, p0, p1, c0, SCRATCH[name][1][1] if c1 is None else c1, st)


def M(b0, b1, r0, r1):
    return ("m", "Mall", r0, r1, b0, b1, 1)


def D(name, s0=0, s1=8):
    return ("d", name, s0, s1, 0, 1, 1)


def E(name, p0=0, p1=128, c0=None, c1=None):
    return ("e", name, p0, p1, c0, c1, 1)


def I(win, off):
    return ("i", win, off)


def regions(a):
    if a[0] == "i":
        return [a[1], a[2]]
    return [] if a[0] == "e" else [a]


def meet(a, b):
    return a[1] == b[1] and a[2] < b[3] and b[2] < a[3] and a[4] < b[5] and b[4] < a[5]


def rank_program(g, core, T, topo):
    me = T.rank_of(core)
    if me is None:
        return
    ops = []

    def ap(a):
        if not isinstance(a, tuple):
            return a
        if a[0] == "i":
            return ap(a[1]).indirect(ap(a[2]))
        t = T[a[1]]
        if a[0] == "c":
            return t[a[2]:a[3], a[4]:a[5]] if a[6] == 1 else t[a[2]:a[3], a[4]:a[5]:a[6]]
        if a[0] == "m":
            return t[:, a[4]] if a[5] == a[4] + 1 else t[:, a[4]:a[5], a[2], :]
        if a[0] == "d":
            return t[a[2]] if a[3] == a[2] + 1 else t[a[2]:a[3]]
        return t[a[2]:a[3], :] if a[4] is None else t[a[2]:a[3], a[4]:a[5]]

    def rec(q, fn, out, ins, sem=None, inc=0):
        wr, rd = [], []
        if out[0] == "i":
            wr.append(out[1]); rd.append(out[2])
        else:
            wr += regions(out)
        for a in ins:
            if isinstance(a, tuple):
                rd += regions(a)
        ops.append({"q": q, "fn": fn, "wr": wr, "rd": rd, "sem": sem, "inc": inc})

    def mm(out, l, r, start=True, stop=True):
        rec("P", lambda: g.tensor.matmul(ap(out), ap(l), ap(r), start, stop), out, [l, r])

    def mms(out, pairs, start=True, stop=True):
        for k, (l, r) in enumerate(pairs):
            mm(out, l, r, start and k == 0, stop and k == len(pairs) - 1)

    def cp(out, a):
        rec("V", lambda: g.vector.tensor_copy(ap(out), ap(a)), out, [a])

    def tt(out, a, b, op):
        rec("V", lambda: g.vector.tensor_tensor(ap(out), ap(a), ap(b), op), out, [a, b])

    def ts(out, a, s1, op0, s2=None, op1=None):
        if op1 is None:
            rec("V", lambda: g.vector.tensor_scalar(ap(out), ap(a), ap(s1), None, op0), out, [a, s1])
        else:
            rec("V", lambda: g.vector.tensor_scalar(ap(out), ap(a), ap(s1), ap(s2), op0, op1), out, [a, s1, s2])

    def ms(out, v):
        rec("V", lambda: g.vector.memset(ap(out), v), out, [])

    def act(out, a, fn=F.Identity, bias=0.0, scale=1.0):
        rec("S", lambda: g.scalar.activation(ap(out), ap(a), fn, bias=ap(bias), scale=ap(scale)), out, [a, bias, scale])

    def iota(out, pat, base=0, cm=0, flt=True):
        if flt:
            rec("G", lambda: g.iota(ap(out), pat, base, cm, allow_small_or_imprecise_dtypes=True), out, [])
        else:
            rec("G", lambda: g.iota(ap(out), pat, base, cm), out, [])

    def mark(out, a, pat, base, fill):
        rec("G", lambda: g.affine_select(ap(out), ap(a), pat, A.not_equal, float(fill), base, 1), out, [a])

    def dma(q, out, a, sem):
        eng = {"Y": g.sync, "S": g.scalar, "G": g}[q]
        rec(q, lambda: eng.dma_start(ap(out), ap(a)), out, [a], sem, 16)

    far = [r for r in range(8) if r != me and topo.die(T.cores[r]) != topo.die(core)]
    near = [r for r in range(8) if r != me and topo.die(T.cores[r]) == topo.die(core)]
    peers = []
    while far or near:
        peers += far[:1] + near[:1]
        far, near = far[1:], near[1:]

    def send(pairs, sem):
        trs = []
        for n, (st, ld) in enumerate(pairs):
            for k, r in enumerate(peers):
                en = topo.engines(core, T.cores[r])
                h = len(en) // 2
                m = (1 << en[k]) | (1 << en[k + h]) if len(pairs) == 1 else 1 << en[k + n * h]
                rid, pid = topo.addr(T.cores[r])[:2]
                trs.append((rid, pid, m, st, r, ld))
        fn = lambda: g.remote_dma_fused([RemoteDMATransfer(dst_ids=[DstId(rid=a, pnc=b)], dma_engine_mask=m, remote_sem=T.sem[sem],
                                                           src=T[st][r], dst=T[ld][me]) for a, b, m, st, r, ld in trs],
                                        local_sem=T.sem["sent"])
        ops.append({"q": "G", "fn": fn, "wr": [], "rd": [D(st, r, r + 1) for st, ld in pairs for r in peers], "sem": "sent", "inc": 14, "remote": 1})
        ops.append({"q": "R", "fn": None, "wr": [D(ld, r, r + 1) for st, ld in pairs for r in peers], "rd": [], "sem": sem, "inc": 14})

    B = lambda k, c0=0, c1=512, st=1: V("B%d" % k, c0, c1, st)
    cnames = {}

    def col(n):
        if n not in cnames:
            cnames[n] = len(cnames)
        return V("cols", cnames[n], cnames[n] + 1)

    r0, r1 = 16 * me, 16 * me + 16
    for h in range(2):
        dma("Y", D("stx%d" % h), E("x", 0, 128, 1024 * h, 1024 * h + 1024), "dx%d" % h)
    dma("S", D("sts"), E("sl"), "ds")
    dma("G", D("stp"), E("prey"), "dp")
    for h in range(2):
        dma("Y", D("ldx%d" % h, me, me + 1), E("x", r0, r1, 1024 * h, 1024 * h + 1024), "dxo%d" % h)
    dma("S", D("lds", me, me + 1), E("sl", r0, r1), "dso")
    dma("S", D("ldp", me, me + 1), E("prey", r0, r1), "dpo")
    iota(V("pi", 0, 1), [[0, 1]], 0, 1, False)
    iota(V("i256"), [[0, 2], [1, 128]])
    iota(V("i144"), [[1, 144]])
    iota(V("cgrp"), [[1, 8], [0, 16]])
    send([("sts", "lds"), ("stp", "ldp")], "al")
    send([("stx0", "ldx0")], "ax0")
    send([("stx1", "ldx1")], "ax1")
    iota(V("prow"), [[1, 256]])
    dma("Y", V("SL"), D("lds"), "dsl")
    dma("Y", V("PR"), D("ldp"), "dpr")
    for h in range(2):
        dma("Y", V("TT", 1024 * h, 1024 * h + 1024), D("ldx%d" % h), "dt%d" % h)
    for h in range(2):
        for b in DMA0:
            o = 2048 * b + 1024 * h
            dma("Y", V("TT", o, o + 1024, p1=128 - 16 * b), D("ldx%d" % h, b, 8), "dT0")
            dma("Y", V("TT", o, o + 1024, p0=128 - 16 * b), D("ldx%d" % h, 0, b), "dT0")

    ms(V("z32"), 0.0); ms(V("zb"), 0.0); ms(V("on16"), 1.0); ms(V("onb"), 1.0)
    for n in range(3):
        ms(V("Perm", 136 * n, 136 * n + 8), 0.0)
    ms(V("qrow", p1=1), 0.25); ms(V("zrow", p1=1), 0.0); ms(V("Zs"), 0.0)
    pi = V("pi", 0, 1)
    pj = lambda k: V("pj", k, k + 1)
    ts(pj(0), pi, 4, A.arith_shift_right)
    ts(pj(1), pi, 7, A.bitwise_and)
    ts(pj(2), pi, 15, A.bitwise_and)
    ts(pj(3), pi, 4, A.arith_shift_right, 1, A.bitwise_and)
    ts(pj(4), pi, 6, A.arith_shift_right)
    ts(pj(5), pi, 31, A.bitwise_and)
    for n in ("grp", "j", "i", "sd0", "sd1", "p31"):
        col(n)
    cp(V("cols", 0, 6), V("pj", 0, 6))
    cp(col("p"), pi)
    ts(V("IW"), V("i256"), col("p"), A.is_equal)
    ts(col("mlo"), col("i"), 8.0, A.is_lt)
    ts(col("mhi"), col("i"), 8.0, A.is_ge)
    ts(col("m8"), col("i"), 8.0, A.is_equal)
    ts(col("mlo128"), col("i"), 8.0, A.is_lt, 128.0, A.mult)
    ts(col("rot"), col("grp"), -2048.0, A.mult, 16384.0, A.add)
    ts(col("g15"), col("grp"), 16.0, A.mult, 15.0, A.add)
    ts(col("psc"), col("grp"), 3.5, A.is_lt, 0.5, A.mult)
    ts(col("pbi"), col("grp"), 3.5, A.is_gt, 127.5, A.mult)
    ts(col("w4"), col("p31"), 24.0, A.is_ge, col("sd1"), A.mult)
    ts(V("G8"), V("i144", 0, 8), col("grp"), A.is_equal, -2048.0, A.mult)
    ts(V("blk"), V("cgrp"), col("grp"), A.is_equal)
    ts(col("psc"), col("psc"), 0.5, A.add)
    ts(col("thr"), col("g15"), -15.0, A.add, col("mlo"), A.mult)
    ts(col("rot0"), col("grp"), -2048.0, A.mult)
    ts(col("w4"), col("w4"), -32.0, A.mult, 64.0, A.add)
    ts(V("BWp"), V("i144"), col("g15"), A.is_equal)
    ts(V("BWb"), V("i144"), col("g15"), A.is_equal)
    ts(V("BWn"), V("i144"), col("g15"), A.is_equal, -1.0, A.mult)
    cp(V("G8h"), V("G8"))
    for r in range(8):
        ts(V("KR", 128 * r, 128 * r + 128), V("on16"), V("G8", r, r + 1), A.mult)
    I0, Iup, Idn = V("IW", 0, 128), V("IW", 8, 136), V("IW", 120, 248)
    SM = lambda k: V("SM", 128 * k, 128 * k + 128)
    OH, OL, S1, L1, H0, H1 = [SM(k) for k in range(6)]
    act(V("I8"), I0, scale=0.125)
    act(V("Ih"), I0, scale=0.5)
    for o, a, c in ((OH, I0, "mlo"), (OL, Iup, "mhi"), (S1, Idn, "mlo"), (L1, I0, "mhi"), (H0, I0, "mlo128"), (H1, Idn, "mlo128")):
        act(o, a, scale=col(c))
    WW = lambda y, k: V("WW", 384 * int(y) + 128 * k, 384 * int(y) + 128 * k + 128)

    def side(y):
        sd = col("sd" + y)
        ts(col("sig" + y), sd, -256.0, A.mult, 128.0, A.add)
        ts(col("q" + y), sd, 8.0, A.mult, col("j"), A.add)
        ts(col("be" + y), sd, 9.0, A.mult, col("j"), A.add)
        ts(col("cA" + y), sd, -1024.0, A.mult, 1024.0, A.add)
        ts(col("nb" + y), col("j"), -1920.0, A.mult, -1920.0, A.add)
        ts(col("q" + y), col("q" + y), col("mlo"), A.mult)
        ts(col("be" + y), col("be" + y), -8.0, A.add, col("mlo128"), A.mult)
        ts(col("s1" + y), col("cA" + y), col("mlo"), A.mult)
        ts(col("s3" + y), col("cA" + y), -64.0, A.add, col("m8"), A.mult)
        ts(col("de" + y), col("sig" + y), col("mlo"), A.mult, 1.0 / 16384, A.mult)
        ts(col("nb" + y), sd, 1024.0, A.mult, col("nb" + y), A.add)
        ts(col("be" + y), col("be" + y), 8192.0, A.mult)
        ts(col("s2" + y), col("s1" + y), -0.125, A.mult, col("s3" + y), A.add)

    def side_maps(y):
        act(WW(y, 2), I0, scale=col("de" + y))
        act(WW(y, 0), I0, scale=col("s1" + y))
        act(WW(y, 1), V("blk"), scale=col("s2" + y))

    side("0")
    side_maps("0")
    cp(V("prow16", 0, 256, p1=1), V("prow", p1=1))
    cp(V("prow16", 256, 512, p1=1), V("prow", p1=1))
    ts(V("trow"), V("prow"), 256.0, A.mult, -127.875, A.add)

    def maps(n):
        d = DS[n]
        ra = [r for r in range(8) if r < r ^ d]
        rb = [r ^ d for r in ra]
        pat, base = [[-1, 16]], 0
        for k in range(3):
            if d >> k & 1:
                pat.insert(0, [16 << k, 2]); base -= 16 << k
            elif pat[0][0] < 0 and -pat[0][0] * pat[0][1] == 16 << k:
                pat[0] = [pat[0][0], pat[0][1] * 2]
            else:
                pat.insert(0, [-(16 << k), 2])
        mark(V("Perm", 136 * n + 8, 136 * n + 136), V("z32", 0, 128), pat, base, 1)

        def lay(buf, c0, w, src, rs, pat, base, fill):
            st = rs[1] - rs[0]
            if all(rs[p] == rs[0] + st * p for p in range(4)):
                o = V(buf, c0, c0 + 4 * w)
                mark(o, V(src, 0, 4 * w) if src else o, pat + [[-16 * st, 4]], base - 16 * rs[0], fill)
            else:
                for p in range(4):
                    o = V(buf, c0 + p, c0 + 4 * w, 4)
                    mark(o, V(src, 0, w) if src else o, pat, base - 16 * rs[p], fill)
        pa, pb = [[-1, 8], [0, 8]], [[0, 8], [-1, 8]]
        lay("D2", 256 * n, 64, "zb", ra, pa, 0, 128)
        lay("D2", 256 * n, 64, None, ra, pa, -8, 1)
        lay("D2", 256 * n, 64, None, rb, pb, 0, -128)
        lay("D2", 256 * n, 64, None, rb, pb, -8, -1)
        lay("KD", 512 * n, 64, "z32", ra, pa, 0, 1)
        for s, rs in enumerate((ra, rb)):
            lay("KD", 512 * n + 256 + 128 * s, 32, "z32", rs, [[0, 4], [-1, 8]], 0, 1)
        lay("KD", 512 * n, 64, None, rb, pb, 0, -1)
        for base in (-1, 7):
            for s, rs in enumerate((ra, rb)):
                lay("KD", 512 * n + 256 + 128 * s, 32, None, rs, [[-1, 4], [-1, 8]], base, -1)

    DGp = lambda n, k: V("DGp", 384 * n + 128 * k, 384 * n + 128 * k + 128)
    KD = lambda buf, n, p: V(buf, 512 * n + p, 512 * n + 512, 4)
    D2 = lambda n, h: V("D2", 256 * n + h, 256 * n + 256, 2)

    def maps_a(n):
        act(DGp(n, 0), V("Perm", 136 * n, 136 * n + 128), scale=col("mlo"))
        act(DGp(n, 1), V("Perm", 136 * n + 8, 136 * n + 136), scale=col("mhi"))
        act(DGp(n, 2), V("Perm", 136 * n + 8, 136 * n + 136), scale=-1.0)

    def maps_b(n, bank):
        for h in range(2):
            mm(B(bank, 128 * h, 128 * h + 128), D2(n, h), WW("01"[min(n, 1)], 2))
        act(V("CM", 256 * n, 256 * n + 256), B(bank, 0, 256))

    def maps_c(n):
        act(V("KDb"), V("KD", 512 * n, 512 * n + 512))

    def maps_d(n, bank):
        for p in range(4):
            mms(B(bank, 128 * p, 128 * p + 128), [(KD("KDb", 0, p), OH), (KD("KDb", 0, p), DGp(n, 0))])
        act(V("KC", 512 * n, 512 * n + 512), V("KD", 512 * n, 512 * n + 512), scale=col("be" + "01"[min(n, 1)]))
        act(V("RM", 512 * n, 512 * n + 512), B(bank), scale=col("w4"))

    for n in range(3):
        maps(n)

    def table(n, chunks):
        by_dma = {(ch, b) for k, (k0, bs) in DMAB.items() for ch in range(k0, k + 1) for b in bs}
        jobs = [(ch, b) for ch in range(4) for b in range(1, 8) if (b not in DMA0 if n == 0 else (ch, b) not in by_dma)]
        for k, (ch, b) in enumerate(jobs):
            if ch not in chunks:
                continue
            mm(B(k % 6), V("IW", 16 * b, 16 * b + 128), V("TT", 512 * ch, 512 * ch + 512))
            o = V("TT", 2048 * b + 512 * ch, 2048 * b + 512 * ch + 512)
            if k >= NV[n] and (k - NV[n]) % 2 == 0:
                cp(o, B(k % 6))
            else:
                act(o, B(k % 6))

    maps_a(0)
    ts(V("t1"), V("SL"), col("rot"), A.add)
    ts(V("t4"), V("SL"), 7, A.arith_shift_right)
    ts(V("t2"), V("t1"), 16383, A.bitwise_and)
    ts(V("t3"), V("SL"), 127, A.bitwise_and)
    cp(V("offU"), V("t2"))
    table(0, range(4))
    TW = V("TT")
    ends = [sum(OUTW[:k + 1]) for k in range(len(OUTW))]
    BW = lambda s, a: V(s, 15 - a, 143 - a)
    row = lambda r: B(r // 2, 256 * (r % 2), 256 * (r % 2) + 256)
    for n in range(3):
        y = "01"[min(n, 1)]
        for h in range(2):
            cp(V("X", 512 * h, 512 * h + 512), I(TW, V("offU", 32 * h, 32 * h + 32)))
            act(V("X", 1024 + 512 * h, 1536 + 512 * h), I(TW, V("offU", 64 + 32 * h, 96 + 32 * h)))
        if n == 0:
            cp(V("dh"), V("t4")); cp(V("dl"), V("t3")); cp(V("prU"), V("PR"))
        for k in range(4):
            mm(B(k), V("on16", p1=1), V("prow16", p1=1), True, False)
        for h in (0, 2, 1, 3):
            mms(B(4, 64 * h, 64 * h + 64), [(V("I8"), V("X", 512 * h + j, 512 * h + 512, 8)) for j in range(8)])
        cp(V("C16"), B(4, 0, 256))
        for k in range(2):
            mms(B(5, 8 * k, 8 * k + 8), [(V("prow16", 128 * k, 128 * k + 128, p1=1), V("on16", 0, 8, p1=1)),
                                         (V("C16", 128 * k, 128 * k + 128), V("G8h"))])
        for r in (4, 5, 0, 1, 6, 7, 2, 3):
            mm(row(r), V("KR", 128 * r, 128 * r + 128), V("C16"), False, r % 2 == 1)
        if n == 0:
            mms(B(6, 0, 128), [(OH, V("dh")), (S1, V("dl"))])
            mms(B(6, 128, 256), [(OL, V("dh")), (L1, V("dl"))])
        act(V("neg"), B(5, 0, 16), scale=-1.0)
        tt(V("Z"), B(4, 0, 256), V("trow"), A.add)
        for k in range(2):
            for r in range(4):
                ts(M(16 * k, 16 * k + 16, r, r + 1), row(r), V("neg", 8 * k + r, 8 * k + r + 1), A.add, 0.0, A.is_gt)
        for k in range(2):
            for r in range(4, 8):
                act(M(16 * k, 16 * k + 16, r, r + 1), row(r), F.Sign, bias=V("neg", 8 * k + r, 8 * k + r + 1))
        m1 = lambda j: tt(V("M1", 256 * j, 256 * j + 256), V("X", j, 2048, 8), B(4, 0, 256), A.max)
        for j in range(3):
            m1(j)
        mm(B(5, 16, 32), V("on16", p1=1), V("zrow", p1=1), True, False)
        for k in range(2):
            for b in range(16):
                mm(B(5, 16 + b, 17 + b), M(16 * k + b, 16 * k + b + 1, 0, 8), V("onb", 0, 1), False, k + b == 16)
        ts(V("posU"), B(5, 16, 32), col("psc"), A.mult, col("pbi"), A.add)
        cp(I(V("Zs"), V("posU")), V("Z"))
        ts(V("od"), V("Zs"), 256 * MAGIC, A.add, -256 * MAGIC, A.add)
        for j in range(3, 8):
            m1(j)
        if n == 0:
            act(V("IDd", 0, 256, 2), B(6, 0, 128))
            act(V("IDd", 1, 256, 2), B(6, 128, 256))
            maps_c(0)
            maps_b(0, 7)
        for j in range(8):
            mm(row(j), I0, V("X", j, 2048, 8))
        mms(B(7, 0, 256), [(V("Perm", 136 * n + 8, 136 * n + 136), V("Zs")), (DGp(n, 2), V("od"))])
        act(V("Cps"), B(7, 0, 256), bias=127.875)
        act(V("Cp"), I(V("Cps"), V("posU")))
        mms(B(5, 32, 48), [(BW("BWb", a), V("od", a, 256, 16)) for a in range(16)])
        ts(V("ordU"), B(5, 32, 48), 1.0 / 4096, A.mult)
        act(V("IDs"), I(V("IDd"), V("ordU")))
        mms(B(6, 0, 256), [(BW("BWp", j), V("M1", 256 * j, 256 * j + 256)) for j in range(4)], stop=False)
        for h in range(2):
            mm(B(4, 256 * h, 256 * h + 256), D2(n, h), V("IDs"))
        mms(B(6, 0, 256), [(BW("BWp", j), V("M1", 256 * j, 256 * j + 256)) for j in range(4, 8)], start=False, stop=False)
        act(V("AB"), B(4), F.Abs)
        act(V("Eq"), V("AB"), F.Relu, bias=1.0, scale=-1.0)
        for j in range(8):
            tt(V("M2", 256 * j, 256 * j + 256), row(j), V("Cp"), A.max)
        for j in range(8):
            mm(B(6, 0, 256), BW("BWn", j), V("M2", 256 * j, 256 * j + 256), False, j == 7)
            if j == 6:
                mms(B(7, 0, 256), [(V("CM", 256 * n + 128 * h, 256 * n + 128 * h + 128), V("Eq", 256 * h, 256 * h + 256)) for h in range(2)])
                act(V("com"), B(7, 0, 256), bias=col("m8"))
        if n == 0:
            maps_d(0, 4)
        ts(V("Kf"), B(6, 0, 256), col("sig" + y), A.mult, col("q" + y), A.add)
        cp(V("Ks"), I(V("Kf"), V("ordU")))
        if n == 0:
            side("1")
        for p in range(4):
            mm(B(p, 0, 256), KD("KC", n, p), V("com"), True, False)
        sg = lambda p: V("sg", 256 * p, 256 * p + 256)
        rk = lambda p: mm(B(5, 0, 256), V("RM", 512 * n + 128 * p, 512 * n + 128 * p + 128), sg(p), p == 0, p == 3)
        vw = lambda bank, own, k: mms(B(bank, 0, 256), [(own, V("IDs")), (DGp(n, k), V("IDs")), (WW(y, 0), V("com")), (WW(y, 1), V("com"))])
        for p in range(4):
            mm(B(p, 0, 256), KD("KD", n, p), V("Ks"), False, True)
            if p % 2 == 0:
                act(sg(p), B(p, 0, 256), F.Sign)
            else:
                ts(sg(p), B(p, 0, 256), -1.0, A.max, 1.0, A.min)
        for p in range(4):
            rk(p)
        vw(7, OH, 0)
        vw(4, OL, 1)
        ts(V("Tq"), B(5, 0, 256), 64.0, A.is_ge, col("cA" + y), A.mult)
        tt(V("Rq"), B(5, 0, 256), V("Tq"), A.add)
        tt(V("vv", 0, 256), B(7, 0, 256), V("Rq"), A.add)
        tt(V("vv", 256, 512), B(4, 0, 256), V("Rq"), A.add)
        if n == 0:
            side_maps("1")
        if n < 2:
            maps_a(n + 1)
            maps_c(n + 1)
        for j in range(8):
            ts(V("FF", 512 * j, 512 * j + 512), V("vv"), 128.0 * j, A.max, 128.0 * j + 128, A.min)
            for k in range(2):
                mm(B(6, 0, 256), BW("BWp", 8 * k + j), V("FF", 512 * j + 256 * k, 512 * j + 256 * k + 256), j + k == 0, j + k == 8)
        if n < 2:
            maps_b(n + 1, 0)
            maps_d(n + 1, 1)
        ts(V("Ns"), B(6, 0, 256), col("nb" + y), A.add)
        cp(V("IDd"), I(V("Ns"), V("posU")))
        ev, od = V("IDd", 0, 256, 2), V("IDd", 1, 256, 2)
        ts(V("wr"), V("IDd"), col("thr"), A.is_lt, 128.0, A.mult)
        ids = [(H0, ev), (OL, ev), (H1, od), (L1, od)]
        mms(B(5, 0, 128), ids + [(H0, V("wr", 0, 256, 2)), (H1, V("wr", 1, 256, 2))])
        ts(V("offU"), B(5, 0, 128), col("rot0"), A.add)
        if n == 2:
            mms(B(4, 0, 128), ids)
            act(V("YL"), B(4, 0, 128))
            dma("Y", D("stl"), V("YL"), "dl")
            dma("Y", D("ldl", me, me + 1), V("YL", p0=r0, p1=r1), "dlo")
            send([("stl", "ldl")], "ayl")
        ts(V("Xn", 0, 1024), I(TW, V("offU", 0, 64)), 2048.5, A.add)
        act(V("Xn", 1024, 2048), I(TW, V("offU", 64, 128)), bias=2048.5)
        xh = lambda ch: V("XH", 512 * ch, 512 * ch + 512)
        by_s = (1, 3) if n < 2 else (1, 2, 3)
        bank = {1: 6, 2: 5, 3: 7}
        for ch in by_s:
            act(xh(ch), I(V("Xn"), V("prU", 32 * ch, 32 * ch + 32)), bias=-2048.5)
        for ch in range(4):
            c0, c1 = 512 * ch, 512 * ch + 512
            if ch + 1 in by_s:
                mms(B(bank[ch + 1]), [(V("on16", p1=1), V("qrow", p1=1)), (V("Ih"), V("TT", c1, c1 + 512)), (V("Ih"), xh(ch + 1))])
            if ch not in by_s:
                tt(V("N16", c0, c1), I(V("Xn"), V("prU", 32 * ch, 32 * ch + 32)), V("TT", c0, c1), A.add)
                ts(V("TT", c0, c1), V("N16", c0, c1), -2048.0, A.add, 0.5, A.mult)
            else:
                ts(V("TT", c0, c1), B(bank[ch]), MAGIC, A.add, -MAGIC, A.add)
            if n < 2 and ch in DMAB:
                k0, bs = DMAB[ch]
                for b in bs:
                    s, o = 16 * b, 2048 * b
                    dma("Y", V("TT", o + 512 * k0, o + c1, p1=128 - s), V("TT", 512 * k0, c1, p0=s), "dT%d" % (n + 1))
                    dma("Y", V("TT", o + 512 * k0, o + c1, p0=128 - s), V("TT", 512 * k0, c1, p1=s), "dT%d" % (n + 1))
            if n < 2 and ch == 1:
                table(n + 1, (0, 1))
            if n == 2 and c1 in ends:
                k = ends.index(c1)
                dma("Y", D("sto%d" % k), V("TT", c1 - OUTW[k], c1), "do%d" % k)
                dma("Y", D("ldo%d" % k, me, me + 1), V("TT", c1 - OUTW[k], c1, p0=r0, p1=r1), "doo%d" % k)
                send([("sto%d" % k, "ldo%d" % k)], "ao%d" % k)
        if n < 2:
            table(n + 1, (2, 3))
    dma("Y", E("yl"), D("ldl"), "dyl")
    for k in range(len(OUTW)):
        dma("G", E("yx", 0, 128, ends[k] - OUTW[k], ends[k]), D("ldo%d" % k), "dy%d" % k)

    hist = {}
    for n, o in enumerate(ops):
        deps = set()
        for a, w in [(a, True) for a in o["wr"]] + [(a, False) for a in o["rd"]]:
            bank = SCRATCH[a[1]][0] == "psum"
            for m, b, w2 in hist.get(a[1], []):
                q2 = ops[m]["q"]
                if q2 == "P" and o["q"] == "P":
                    continue
                if (bank and q2 != o["q"]) or ((w or w2) and meet(a, b)):
                    deps.add(m)
        for a in o["wr"]:
            hist.setdefault(a[1], []).append((n, a, True))
        for a in o["rd"]:
            hist.setdefault(a[1], []).append((n, a, False))
        last = {}
        for m in deps:
            key = ops[m]["sem"] or ops[m]["q"]
            last[key] = max(last.get(key, -1), m)
        o["deps"] = sorted(last.values())
    seen = {}
    for n, o in enumerate(ops):
        keep = []
        for m in o["deps"]:
            key = (o["q"], ops[m]["sem"] or ops[m]["q"])
            if seen.get(key, -1) < m:
                seen[key] = m
                keep.append(m)
                ops[m]["need"] = True
        o["deps"] = keep
    total = {}
    for o in ops:
        if o["sem"]:
            total[o["sem"]] = total.get(o["sem"], 0) + o["inc"]
        elif o.get("need"):
            total["c" + o["q"]] = o["cnt"] = total.get("c" + o["q"], 0) + 1
    eng = {"V": g.vector, "S": g.scalar, "P": g.tensor, "G": g, "Y": g.sync}
    waited = {}
    for o in ops:
        if o["q"] == "R":
            continue
        for m in o["deps"]:
            s = ops[m]["sem"] or "c" + ops[m]["q"]
            v = total[s] if ops[m]["sem"] else ops[m]["cnt"]
            if waited.get((o["q"], s), 0) < v:
                eng[o["q"]].wait_ge(T.sem[s], v)
                waited[(o["q"], s)] = v
        h = o["fn"]()
        if o.get("remote"):
            continue
        if o["sem"]:
            h.then_inc(T.sem[o["sem"]], 16)
        elif o.get("need"):
            h.then_inc(T.sem["c" + o["q"]], 1)
    for s, v in total.items():
        if max([waited.get((q, s), 0) for q in eng]) < v:
            g.wait_ge(T.sem[s], v)
